import numpy as np
import ml_dtypes


def mxq(x, axis, fmt="e4m3"):
    dtype, down = {"e4m3": (ml_dtypes.float8_e4m3fn, 7), "e5m2": (ml_dtypes.float8_e5m2, 14)}[fmt]
    v = np.moveaxis(np.asarray(x, np.float32).astype(ml_dtypes.bfloat16).astype(np.float64), axis, -1)
    blocks = v.reshape(v.shape[:-1] + (-1, 32))
    amax = np.abs(blocks).max(-1, keepdims=True)
    byte = np.maximum(np.where(amax > 0, np.frexp(amax)[1] - 1 + 127, 0) - down, 1)
    scale = np.exp2(byte - 127.0)
    codes = (blocks / scale).astype(np.float32).astype(dtype).astype(np.float64)
    return np.moveaxis((codes * scale).reshape(v.shape), -1, axis)


WIDE = False


def mx_kscale(k):
    if not WIDE:
        return np.ones(k)
    levels = np.array([10, -10, 5, -5, 0])
    if k % 512:
        return np.exp2(np.random.permutation(np.resize(levels, k // 32))).repeat(32)
    a = np.empty((k // 512, 16))
    for p in range(k // 512):
        a[p, :8] = np.random.permutation(np.resize(levels, 8))
        for g in range(8):
            far = levels[np.abs(levels - a[p, g]) >= 10]
            a[p, g + 8] = far[np.random.randint(len(far))]
    return np.exp2(a.ravel()).repeat(32)


def f64(x):
    return np.asarray(x).astype(np.float64)


def striped(idx):
    return np.tile(idx.reshape(-1, 16).T, (8, 1)).astype(np.uint16)


def unstriped(offs):
    return offs[:16].T.reshape(-1).astype(np.int64)


def striped8(idx):
    return np.concatenate([x.reshape(-1, 16).T for x in idx]).astype(np.uint16)


def runs(offs, k):
    lists = np.stack([offs[16 * r : 16 * r + 16].T.reshape(-1) for r in range(8)]).astype(np.int64)
    return lists[np.arange(k) % 512 // 64]


def pack_weight(w):
    k, n = w.shape
    w = f64(np.asarray(w, np.float32).astype(ml_dtypes.bfloat16)).reshape(k // 32, 32, n)
    amax = np.abs(w).max(1)
    byte = np.clip(np.where(amax > 0, np.frexp(amax)[1] - 1 + 127 - 7, 1), 1, 254)
    scaled = (w * np.exp2(127.0 - byte)[:, None, :]).reshape(k, n).astype(np.float32)
    words = np.ascontiguousarray(scaled.reshape(k // 512, 128, 4, n).transpose(0, 1, 3, 2)).astype(ml_dtypes.float8_e4m3fn).view(np.uint8)
    return words, np.ascontiguousarray(byte.astype(np.uint8).reshape(k // 512, 16, n))


def unpack_weight(words, scales):
    g, p, n, _ = words.shape
    vals = np.ascontiguousarray(words).view(ml_dtypes.float8_e4m3fn).astype(np.float64) * np.repeat(np.exp2(scales.astype(np.float64) - 127.0), 8, axis=1)[..., None]
    return vals.transpose(0, 1, 3, 2).reshape(g * 512, n)


K, T, S, N, G, H, U = 512, 2048, 512, 512, 2048, 512, 512


def setup_inputs():
    n = np.random.standard_normal
    s = mx_kscale(K)[:, None]
    u = mx_kscale(H)
    packed_xT = pack_weight(n((K, T)) * s)
    packed_dT = pack_weight(n((K, G)) / s)
    return {
        "x_words": packed_xT[0],
        "x_scales": packed_xT[1],
        "d_words": packed_dT[0],
        "d_scales": packed_dT[1],
        "temp": np.random.uniform(0.3, 1.5, (H, U)).astype(np.float32),
        "gn": (np.random.uniform(0.5, 1.5, (H, 1)) * u[:, None]).astype(np.float32),
        "w1": (n((H, N)) / np.sqrt(H) / u[:, None]).astype(np.float32),
        "offs": striped(np.random.permutation(T)[:S]),
        "kidx": striped8(np.random.randint(0, G, (8, H))),
        "task": striped8(np.stack([np.random.permutation(U)[(U * np.random.uniform(0, 1, S) ** 4).astype(np.int64)] for _ in range(8)])),
    }


def reference(x_words, x_scales, d_words, d_scales, temp, gn, w1, offs, kidx, task):
    d_kidx = unpack_weight(d_words, d_scales)[np.arange(K)[:, None], runs(kidx, K)]
    xq = unpack_weight(x_words, x_scales)[:, unstriped(offs)]
    s = 0.0625 * (d_kidx.T @ xq)
    z = f64(gn) * (np.tanh(s * (f64(temp)[np.arange(H)[:, None], runs(task, H)])))
    return mxq(f64(w1), 0, "e4m3").T @ mxq(z, 0, "e4m3")

@@ -1,0 +1,190 @@
+from contextlib import ExitStack
+
+import concourse.mybir as mybir
+
+F32 = mybir.dt.float32
+BF16 = mybir.dt.bfloat16
+I32 = mybir.dt.int32
+U32 = mybir.dt.uint32
+U16 = mybir.dt.uint16
+U8 = mybir.dt.uint8
+FP8X4 = mybir.dt.float8_e4m3fn_x4
+ACT = mybir.ActivationFunctionType
+MULT = mybir.AluOpType.mult
+
+P = 128
+PACK = 4
+TABLE = 2048
+S = 512
+H = 512
+N = 512
+U = 512
+HALF = 256
+CHUNKS = ((0, 256), (256, 128), (384, 128))
+FLOPS = 2 * 512 * H * S + 2 * H * N * S
+
+
+def tile_picked_temper_tanh_p_kernel(
+    tc, x_words, x_scales, d_words, d_scales, temp, gn, w1, offs, kidx, task, out
+):
+    nc = tc.nc
+    with ExitStack() as ctx:
+        lists = ctx.enter_context(tc.tile_pool(name="lists", bufs=1))
+        sb = ctx.enter_context(tc.tile_pool(name="sb", bufs=1))
+        ps = ctx.enter_context(tc.psum_pool(name="ps", bufs=1))
+
+        kidx_sb = lists.tile([P, H // 16], U16, name="kidx_sb")
+        offs_sb = lists.tile([P, S // 16], U16, name="offs_sb")
+        task_sb = lists.tile([P, S // 16], U16, name="task_sb")
+        dsc_win = sb.tile([P, TABLE], U8, name="dsc_win", align_bytes=64)
+        xsc_win = sb.tile([P, TABLE], U8, name="xsc_win", align_bytes=64)
+        spread = [16, 8, TABLE // 4]
+        nc.sync.dma_start(kidx_sb[:], kidx)
+        nc.sync.dma_start(dsc_win[:].bitcast(I32), d_scales[0].bitcast(I32).unsqueeze(1).to_broadcast(spread))
+        nc.sync.dma_start(offs_sb[:], offs)
+        nc.sync.dma_start(xsc_win[:].bitcast(I32), x_scales[0].bitcast(I32).unsqueeze(1).to_broadcast(spread))
+        nc.sync.dma_start(task_sb[:], task)
+        gn_sb = sb.tile([P, PACK], F32, name="gn_sb")
+        nc.sync.dma_start(gn_sb[:], gn.rearrange("(p t) o -> p (t o)", t=PACK))
+        warm = sb.tile([P, 2], F32, name="warm")
+        nc.vector.memset(warm[:, 0:1], 0.0)
+        nc.scalar.activation(warm[:, 1:2], warm[:, 0:1], ACT.Tanh)
+
+        dw_win = sb.tile([P, TABLE], I32, name="dw_win", tag="dw_then_w", align_bytes=64)
+        xw_win = sb.tile([P, TABLE], I32, name="xw_win", align_bytes=64)
+        nc.sync.dma_start(dw_win[:], d_words[0].rearrange("p n t -> p (n t)").bitcast(I32))
+        nc.sync.dma_start(xw_win[:], x_words[0].rearrange("p n t -> p (n t)").bitcast(I32))
+
+        temp_rows = temp.rearrange("(p t) u -> p t u", t=PACK)
+        temp_win = []
+        for t in range(PACK):
+            win = sb.tile([P, U], F32, name=f"temp_win{t}", align_bytes=64)
+            nc.sync.dma_start(win[:], temp_rows[:, t, :])
+            temp_win.append(win)
+
+        dsc_got = sb.tile([P, H], U8, name="dsc_got", align_bytes=64)
+        xsc_got = sb.tile([P, S], U8, name="xsc_got", align_bytes=64)
+        planes = sb.tile([P, H + S], U8, name="planes", align_bytes=64)
+        nc.vector.tensor_copy(dsc_got[:], dsc_win[:].indirect(kidx_sb[:]))
+        nc.vector.tensor_copy(xsc_got[:], xsc_win[:].indirect(offs_sb[:]))
+        nc.vector.tensor_copy(
+            planes[:, 0:H].rearrange("p (t m) -> p m t", t=PACK),
+            dsc_got[:].rearrange("p (m t) -> p m t", t=PACK),
+        )
+        nc.vector.tensor_copy(planes[:, H : H + S].bitcast(I32), xsc_got[:].bitcast(I32))
+        for r in range(1, PACK):
+            nc.scalar.dma_start(planes[r:P:32, :].bitcast(I32), planes[8 * r : P : 32, :].bitcast(I32))
+
+        dw_got = sb.tile([P, H], U32, name="dw_got", tag="dw_got", align_bytes=64)
+        dw_dealt = sb.tile([P, H], U32, name="dw_dealt", align_bytes=64)
+        nc.vector.tensor_copy(dw_got[:], dw_win[:].bitcast(U32).indirect(kidx_sb[:]))
+        nc.vector.tensor_copy(
+            dw_dealt[:].rearrange("p (t m) -> p m t", t=PACK),
+            dw_got[:].rearrange("p (m t) -> p m t", t=PACK),
+        )
+
+        w_rows = w1.rearrange("(p t) m -> p t m", t=PACK)
+        w_raw = []
+        for h, held_by in enumerate(("dw_then_w", "dw_got")):
+            raw = sb.tile([P, PACK, HALF], F32, name=f"w_raw{h}", tag=held_by, align_bytes=64)
+            nc.sync.dma_start(raw[:], w_rows[:, :, h * HALF : (h + 1) * HALF])
+            w_raw.append(raw)
+
+        s_sb = []
+        for h in range(S // HALF):
+            xw_got = sb.tile([P, HALF], U32, name=f"xw_got{h}", align_bytes=64)
+            nc.vector.tensor_copy(
+                xw_got[:], xw_win[:].bitcast(U32).indirect(offs_sb[:, h * HALF // 16 : (h + 1) * HALF // 16])
+            )
+            s_half = sb.tile([P, PACK, HALF], F32, name=f"s_half{h}", align_bytes=64)
+            per_bank = h + 1
+            for b in range(PACK // per_bank):
+                bank = ps.tile([P, per_bank, HALF], F32, name=f"s_bank{h}{b}", tag=f"bank{4 * h + b}")
+                for e in range(per_bank):
+                    t = per_bank * b + e
+                    nc.tensor.matmul_mx(
+                        out=bank[:, e, :],
+                        lhsT=dw_dealt[:, t * P : (t + 1) * P].bitcast(FP8X4),
+                        lhsT_scale=planes[:, t * P : (t + 1) * P],
+                        rhs=xw_got[:].bitcast(FP8X4),
+                        rhs_scale=planes[:, H + h * HALF : H + (h + 1) * HALF],
+                        start=True,
+                        stop=True,
+                    )
+                nc.scalar.copy(s_half[:, per_bank * b : per_bank * (b + 1), :], bank[:])
+            s_sb.append(s_half)
+
+        def temper(c, held_by):
+            j0, n = CHUNKS[c]
+            s_half, lo = s_sb[j0 // HALF], j0 % HALF
+            y = sb.tile([P, PACK, n], F32, name=f"y{c}", tag=held_by, align_bytes=64)
+            th = sb.tile([P, PACK, n], F32, name=f"th{c}", align_bytes=64)
+            zt = sb.tile([P, PACK, n], BF16, name=f"zt{c}", align_bytes=64)
+            for t in range(PACK):
+                nc.vector.tensor_tensor(
+                    y[:, t, :],
+                    temp_win[t][:].indirect(task_sb[:, j0 // 16 : (j0 + n) // 16]),
+                    s_half[:, t, lo : lo + n],
+                    MULT,
+                )
+                nc.scalar.activation(th[:, t, :], y[:, t, :], ACT.Tanh, scale=0.0625)
+                nc.scalar.activation(zt[:, t, :], th[:, t, :], ACT.Copy, scale=gn_sb[:, t : t + 1])
+            return zt
+
+        def weave(src, n, label):
+            woven = sb.tile([P, n, PACK], BF16, name=f"woven_{label}", tag=f"woven_{label}", align_bytes=64)
+            nc.vector.tensor_copy(
+                woven[:].rearrange("p (c i) t -> p c t i", i=4),
+                src[:].rearrange("p t (c i) -> p c t i", i=4),
+            )
+            return woven
+
+        def quantise(woven, n, label):
+            codes = sb.tile([P, n], U32, name=f"codes_{label}", align_bytes=64)
+            scales = sb.tile([P, n], U8, name=f"scales_{label}", align_bytes=64)
+            nc.vector.quantize_mx(
+                out=codes[:].bitcast(FP8X4), scales=scales[:], in_=woven[:].rearrange("p n t -> p (n t)")
+            )
+            return codes, scales
+
+        out_rows = out.rearrange("(b p) j -> p b j", p=P)
+
+        def project(c, h, z_q, w_q, bank_tag, last=False):
+            j0, n = CHUNKS[c]
+            res = sb.tile([P, 2, n], F32, name=f"res{c}{h}", align_bytes=64)
+            bank = ps.tile([P, 2, n], F32, name=f"o_bank{c}{h}", tag=bank_tag)
+            for e in range(2):
+                nc.tensor.matmul_mx(
+                    out=bank[:, e, :],
+                    lhsT=w_q[0][:, e * P : (e + 1) * P].bitcast(FP8X4),
+                    lhsT_scale=w_q[1][:, e * P : (e + 1) * P],
+                    rhs=z_q[0][:].bitcast(FP8X4),
+                    rhs_scale=z_q[1][:],
+                    start=True,
+                    stop=True,
+                )
+            if last:
+                nc.vector.tensor_copy(res[:], bank[:])
+            else:
+                nc.scalar.copy(res[:], bank[:])
+            nc.sync.dma_start(out_rows[:, 2 * h : 2 * h + 2, j0 : j0 + n], res[:])
+
+        z0 = temper(0, "y0")
+        wa = weave(w_raw[0], HALF, "wa")
+        zw0 = weave(z0, CHUNKS[0][1], "z0")
+        qwa = quantise(wa, HALF, "wa")
+        q0 = quantise(zw0, CHUNKS[0][1], "z0")
+        project(0, 0, q0, qwa, "bank6")
+        z1 = temper(1, "woven_z0")
+        wb = weave(w_raw[1], HALF, "wb")
+        zw1 = weave(z1, CHUNKS[1][1], "z1")
+        qwb = quantise(wb, HALF, "wb")
+        project(0, 1, q0, qwb, "bank7")
+        z2 = temper(2, "woven_wb")
+        q1 = quantise(zw1, CHUNKS[1][1], "z1")
+        project(1, 0, q1, qwa, "bank0")
+        project(1, 1, q1, qwb, "bank1")
+        zw2 = weave(z2, CHUNKS[2][1], "z2")
+        q2 = quantise(zw2, CHUNKS[2][1], "z2")
+        project(2, 0, q2, qwa, "bank2")
+        project(2, 1, q2, qwb, "bank3", last=True)

@@ -31,6 +31,7 @@ def tile_picked_temper_tanh_p_kernel(
     with ExitStack() as ctx:
         lists = ctx.enter_context(tc.tile_pool(name="lists", bufs=1))
         sb = ctx.enter_context(tc.tile_pool(name="sb", bufs=1))
+        shared = ctx.enter_context(tc.tile_pool(name="shared", bufs=1))
         ps = ctx.enter_context(tc.psum_pool(name="ps", bufs=1))
 
         kidx_sb = lists.tile([P, H // 16], U16, name="kidx_sb")
@@ -50,20 +51,22 @@ def tile_picked_temper_tanh_p_kernel(
         nc.vector.memset(warm[:, 0:1], 0.0)
         nc.scalar.activation(warm[:, 1:2], warm[:, 0:1], ACT.Tanh)
 
-        dw_win = sb.tile([P, TABLE], I32, name="dw_win", tag="dw_then_w", align_bytes=64)
+        dw_win = shared.tile([P, TABLE], I32, name="dw_win", align_bytes=64, offset=4096)
         xw_win = sb.tile([P, TABLE], I32, name="xw_win", align_bytes=64)
         nc.sync.dma_start(dw_win[:], d_words[0].rearrange("p n t -> p (n t)").bitcast(I32))
         nc.sync.dma_start(xw_win[:], x_words[0].rearrange("p n t -> p (n t)").bitcast(I32))
 
         temp_rows = temp.rearrange("(p t) u -> p t u", t=PACK)
-        temp_win = []
-        for t in range(PACK):
-            win = sb.tile([P, U], F32, name=f"temp_win{t}", align_bytes=64)
+
+        def load_temp(t, offset):
+            win = shared.tile([P, U], F32, name=f"temp_win{t}", align_bytes=64, offset=offset)
             nc.sync.dma_start(win[:], temp_rows[:, t, :])
-            temp_win.append(win)
+            return win
+
+        temp_win = [load_temp(0, 12288)]
 
         dsc_got = sb.tile([P, H], U8, name="dsc_got", align_bytes=64)
-        xsc_got = sb.tile([P, S], U8, name="xsc_got", align_bytes=64)
+        xsc_got = shared.tile([P, S], U8, name="xsc_got", align_bytes=64, offset=1792)
         planes = sb.tile([P, H + S], U8, name="planes", align_bytes=64)
         nc.vector.tensor_copy(dsc_got[:], dsc_win[:].indirect(kidx_sb[:]))
         nc.vector.tensor_copy(xsc_got[:], xsc_win[:].indirect(offs_sb[:]))
@@ -73,7 +76,9 @@ def tile_picked_temper_tanh_p_kernel(
         )
         nc.vector.tensor_copy(planes[:, H : H + S].bitcast(I32), xsc_got[:].bitcast(I32))
         for r in range(1, PACK):
-            nc.scalar.dma_start(planes[r:P:32, :].bitcast(I32), planes[8 * r : P : 32, :].bitcast(I32))
+            nc.sync.dma_start(planes[r:P:32, :].bitcast(I32), planes[8 * r : P : 32, :].bitcast(I32))
+        temp_win.append(load_temp(1, 0))
+        temp_win.append(load_temp(2, 2048))
 
         dw_got = sb.tile([P, H], U32, name="dw_got", tag="dw_got", align_bytes=64)
         dw_dealt = sb.tile([P, H], U32, name="dw_dealt", align_bytes=64)
@@ -82,61 +87,65 @@ def tile_picked_temper_tanh_p_kernel(
             dw_dealt[:].rearrange("p (t m) -> p m t", t=PACK),
             dw_got[:].rearrange("p (m t) -> p m t", t=PACK),
         )
-
+        temp_win.append(load_temp(3, 4096))
         w_rows = w1.rearrange("(p t) m -> p t m", t=PACK)
-        w_raw = []
-        for h, held_by in enumerate(("dw_then_w", "dw_got")):
-            raw = sb.tile([P, PACK, HALF], F32, name=f"w_raw{h}", tag=held_by, align_bytes=64)
-            nc.sync.dma_start(raw[:], w_rows[:, :, h * HALF : (h + 1) * HALF])
-            w_raw.append(raw)
+        w_raw = [
+            shared.tile([P, PACK, HALF], F32, name="w_raw0", align_bytes=64, offset=6144),
+            sb.tile([P, PACK, HALF], F32, name="w_raw1", tag="dw_got", align_bytes=64),
+        ]
+        for h in range(2):
+            nc.sync.dma_start(w_raw[h][:], w_rows[:, :, h * HALF : (h + 1) * HALF])
 
-        s_sb = []
-        for h in range(S // HALF):
+        banks = [ps.tile([P, 2, HALF], F32, name=f"s_bank{b}", tag=f"bank{b}") for b in range(5)]
+        place = {(0, 0): (0, 0), (1, 0): (1, 0), (2, 0): (2, 0), (3, 0): (2, 1),
+                 (0, 1): (3, 0), (1, 1): (3, 1), (2, 1): (4, 0), (3, 1): (4, 1)}
+        s_ps = {}
+        for h in range(2):
             xw_got = sb.tile([P, HALF], U32, name=f"xw_got{h}", align_bytes=64)
             nc.vector.tensor_copy(
                 xw_got[:], xw_win[:].bitcast(U32).indirect(offs_sb[:, h * HALF // 16 : (h + 1) * HALF // 16])
             )
-            s_half = sb.tile([P, PACK, HALF], F32, name=f"s_half{h}", align_bytes=64)
-            per_bank = h + 1
-            for b in range(PACK // per_bank):
-                bank = ps.tile([P, per_bank, HALF], F32, name=f"s_bank{h}{b}", tag=f"bank{4 * h + b}")
-                for e in range(per_bank):
-                    t = per_bank * b + e
-                    nc.tensor.matmul_mx(
-                        out=bank[:, e, :],
-                        lhsT=dw_dealt[:, t * P : (t + 1) * P].bitcast(FP8X4),
-                        lhsT_scale=planes[:, t * P : (t + 1) * P],
-                        rhs=xw_got[:].bitcast(FP8X4),
-                        rhs_scale=planes[:, H + h * HALF : H + (h + 1) * HALF],
-                        start=True,
-                        stop=True,
-                    )
-                nc.scalar.copy(s_half[:, per_bank * b : per_bank * (b + 1), :], bank[:])
-            s_sb.append(s_half)
-
-        def temper(c, held_by):
-            j0, n = CHUNKS[c]
-            s_half, lo = s_sb[j0 // HALF], j0 % HALF
-            y = sb.tile([P, PACK, n], F32, name=f"y{c}", tag=held_by, align_bytes=64)
-            th = sb.tile([P, PACK, n], F32, name=f"th{c}", align_bytes=64)
-            zt = sb.tile([P, PACK, n], BF16, name=f"zt{c}", align_bytes=64)
             for t in range(PACK):
-                nc.vector.tensor_tensor(
-                    y[:, t, :],
-                    temp_win[t][:].indirect(task_sb[:, j0 // 16 : (j0 + n) // 16]),
-                    s_half[:, t, lo : lo + n],
-                    MULT,
+                b, e = place[t, h]
+                s_ps[t, h] = banks[b][:, e, :]
+                nc.tensor.matmul_mx(
+                    out=s_ps[t, h],
+                    lhsT=dw_dealt[:, t * P : (t + 1) * P].bitcast(FP8X4),
+                    lhsT_scale=planes[:, t * P : (t + 1) * P],
+                    rhs=xw_got[:].bitcast(FP8X4),
+                    rhs_scale=planes[:, H + h * HALF : H + (h + 1) * HALF],
+                    start=True,
+                    stop=True,
                 )
-                nc.scalar.activation(th[:, t, :], y[:, t, :], ACT.Tanh, scale=0.0625)
-                nc.scalar.activation(zt[:, t, :], th[:, t, :], ACT.Copy, scale=gn_sb[:, t : t + 1])
-            return zt
 
-        def weave(src, n, label):
-            woven = sb.tile([P, n, PACK], BF16, name=f"woven_{label}", tag=f"woven_{label}", align_bytes=64)
-            nc.vector.tensor_copy(
-                woven[:].rearrange("p (c i) t -> p c t i", i=4),
-                src[:].rearrange("p t (c i) -> p c t i", i=4),
+        s_sb = [sb.tile([P, PACK, HALF], F32, name=f"s_sb{h}", tag=f"s_sb{h}", align_bytes=64) for h in range(2)]
+        y = {}
+
+        def temper(t, h):
+            looked_up = temp_win[t][:].indirect(task_sb[:, h * HALF // 16 : (h + 1) * HALF // 16])
+            if (t, h) == (0, 0):
+                got = sb.tile([P, HALF], F32, name="tg", align_bytes=64)
+                nc.vector.tensor_copy(got[:], looked_up)
+                nc.vector.tensor_tensor(y[h][:, t, :], s_ps[t, h], got[:], MULT)
+            else:
+                nc.vector.tensor_tensor(y[h][:, t, :], looked_up, s_sb[h][:, t, :], MULT)
+
+        def squash(h, lo, n, label):
+            th = sb.tile([P, n, PACK], F32, name=f"th_{label}", align_bytes=64)
+            nc.scalar.activation(
+                th[:].rearrange("p (c i) t -> p c t i", i=4),
+                y[h][:, :, lo : lo + n].rearrange("p t (c i) -> p c t i", i=4),
+                ACT.Tanh,
+                scale=0.0625,
             )
+            return th
+
+        def weigh(z, th, n):
+            nc.vector.tensor_tensor(z, th[:], gn_sb[:].unsqueeze(1).to_broadcast([P, n, PACK]), MULT)
+
+        def weave(copy, src, n, label):
+            woven = sb.tile([P, n, PACK], BF16, name=f"woven_{label}", tag=f"woven_{label}", align_bytes=64)
+            copy(woven[:].rearrange("p (c i) t -> p c t i", i=4), src.rearrange("p t (c i) -> p c t i", i=4))
             return woven
 
         def quantise(woven, n, label):
@@ -149,7 +158,7 @@ def tile_picked_temper_tanh_p_kernel(
 
         out_rows = out.rearrange("(b p) j -> p b j", p=P)
 
-        def project(c, h, z_q, w_q, bank_tag, last=False):
+        def project(c, h, z_q, w_q, bank_tag, copy):
             j0, n = CHUNKS[c]
             res = sb.tile([P, 2, n], F32, name=f"res{c}{h}", align_bytes=64)
             bank = ps.tile([P, 2, n], F32, name=f"o_bank{c}{h}", tag=bank_tag)
@@ -163,28 +172,39 @@ def tile_picked_temper_tanh_p_kernel(
                     start=True,
                     stop=True,
                 )
-            if last:
-                nc.vector.tensor_copy(res[:], bank[:])
-            else:
-                nc.scalar.copy(res[:], bank[:])
+            copy(res[:], bank[:])
             nc.sync.dma_start(out_rows[:, 2 * h : 2 * h + 2, j0 : j0 + n], res[:])
 
-        z0 = temper(0, "y0")
-        wa = weave(w_raw[0], HALF, "wa")
-        zw0 = weave(z0, CHUNKS[0][1], "z0")
+        vcopy, scopy = nc.vector.tensor_copy, nc.scalar.copy
+        nc.scalar.copy(s_sb[0][:, 1, :], s_ps[1, 0])
+        nc.scalar.copy(s_sb[0][:, 2:4, :], banks[2][:])
+        nc.scalar.copy(s_sb[1][:, 0:2, :], banks[3][:])
+        nc.scalar.copy(s_sb[1][:, 2:4, :], banks[4][:])
+        y[0] = sb.tile([P, PACK, HALF], F32, name="y0", align_bytes=64)
+        for t in range(PACK):
+            temper(t, 0)
+        wa = weave(scopy, w_raw[0][:], HALF, "wa")
+        th0 = [squash(0, 128 * c, 128, f"0{c}") for c in range(2)]
+        y[1] = sb.tile([P, PACK, HALF], F32, name="y1", tag="s_sb0", align_bytes=64)
+        for t in range(PACK):
+            temper(t, 1)
+        wb = weave(scopy, w_raw[1][:], HALF, "wb")
+        th1 = [squash(1, 128 * c, 128, f"1{c}") for c in range(2)]
+        z0 = sb.tile([P, HALF, PACK], BF16, name="z0", align_bytes=64)
+        weigh(z0[:, 0:128, :], th0[0], 128)
+        weigh(z0[:, 128:256, :], th0[1], 128)
         qwa = quantise(wa, HALF, "wa")
-        q0 = quantise(zw0, CHUNKS[0][1], "z0")
-        project(0, 0, q0, qwa, "bank6")
-        z1 = temper(1, "woven_z0")
-        wb = weave(w_raw[1], HALF, "wb")
-        zw1 = weave(z1, CHUNKS[1][1], "z1")
+        q0 = quantise(z0, HALF, "z0")
+        project(0, 0, q0, qwa, "bank5", scopy)
         qwb = quantise(wb, HALF, "wb")
-        project(0, 1, q0, qwb, "bank7")
-        z2 = temper(2, "woven_wb")
-        q1 = quantise(zw1, CHUNKS[1][1], "z1")
-        project(1, 0, q1, qwa, "bank0")
-        project(1, 1, q1, qwb, "bank1")
-        zw2 = weave(z2, CHUNKS[2][1], "z2")
-        q2 = quantise(zw2, CHUNKS[2][1], "z2")
-        project(2, 0, q2, qwa, "bank2")
-        project(2, 1, q2, qwb, "bank3", last=True)
+        project(0, 1, q0, qwb, "bank6", scopy)
+        z1 = sb.tile([P, 128, PACK], BF16, name="z1", align_bytes=64)
+        z2 = sb.tile([P, 128, PACK], BF16, name="z2", align_bytes=64)
+        weigh(z1[:], th1[0], 128)
+        weigh(z2[:], th1[1], 128)
+        q1 = quantise(z1, 128, "z1")
+        project(1, 0, q1, qwa, "bank7", scopy)
+        project(1, 1, q1, qwb, "bank0", vcopy)
+        q2 = quantise(z2, 128, "z2")
+        project(2, 0, q2, qwa, "bank1", scopy)
+        project(2, 1, q2, qwb, "bank2", vcopy)

@@ -20,7 +20,7 @@ H = 512
 N = 512
 U = 512
 HALF = 256
-CHUNKS = ((0, 256), (256, 128), (384, 128))
+CH = 128
 FLOPS = 2 * 512 * H * S + 2 * H * N * S
 
 
@@ -40,13 +40,11 @@ def tile_picked_temper_tanh_p_kernel(
         dsc_win = sb.tile([P, TABLE], U8, name="dsc_win", align_bytes=64)
         xsc_win = sb.tile([P, TABLE], U8, name="xsc_win", align_bytes=64)
         spread = [16, 8, TABLE // 4]
+        nc.vector.memset(xsc_win[:].bitcast(I32), 0)
         nc.sync.dma_start(kidx_sb[:], kidx)
         nc.sync.dma_start(dsc_win[:].bitcast(I32), d_scales[0].bitcast(I32).unsqueeze(1).to_broadcast(spread))
         nc.sync.dma_start(offs_sb[:], offs)
-        nc.sync.dma_start(xsc_win[:].bitcast(I32), x_scales[0].bitcast(I32).unsqueeze(1).to_broadcast(spread))
-        nc.sync.dma_start(task_sb[:], task)
-        gn_sb = sb.tile([P, PACK], F32, name="gn_sb")
-        nc.sync.dma_start(gn_sb[:], gn.rearrange("(p t) o -> p (t o)", t=PACK))
+        nc.sync.dma_start(xsc_win[0:P:8, :].bitcast(I32), x_scales[0].bitcast(I32))
         warm = sb.tile([P, 2], F32, name="warm")
         nc.vector.memset(warm[:, 0:1], 0.0)
         nc.scalar.activation(warm[:, 1:2], warm[:, 0:1], ACT.Tanh)
@@ -56,6 +54,7 @@ def tile_picked_temper_tanh_p_kernel(
         nc.sync.dma_start(dw_win[:], d_words[0].rearrange("p n t -> p (n t)").bitcast(I32))
         nc.sync.dma_start(xw_win[:], x_words[0].rearrange("p n t -> p (n t)").bitcast(I32))
 
+        nc.sync.dma_start(task_sb[:], task)
         temp_rows = temp.rearrange("(p t) u -> p t u", t=PACK)
 
         def load_temp(t, offset):
@@ -88,6 +87,8 @@ def tile_picked_temper_tanh_p_kernel(
             dw_got[:].rearrange("p (m t) -> p m t", t=PACK),
         )
         temp_win.append(load_temp(3, 4096))
+        gn_sb = shared.tile([P, PACK], F32, name="gn_sb", align_bytes=64, offset=10240)
+        nc.sync.dma_start(gn_sb[:], gn.rearrange("(p t) o -> p (t o)", t=PACK))
         w_rows = w1.rearrange("(p t) m -> p t m", t=PACK)
         w_raw = [
             shared.tile([P, PACK, HALF], F32, name="w_raw0", align_bytes=64, offset=6144),
@@ -96,60 +97,59 @@ def tile_picked_temper_tanh_p_kernel(
         for h in range(2):
             nc.sync.dma_start(w_raw[h][:], w_rows[:, :, h * HALF : (h + 1) * HALF])
 
-        banks = [ps.tile([P, 2, HALF], F32, name=f"s_bank{b}", tag=f"bank{b}") for b in range(5)]
-        place = {(0, 0): (0, 0), (1, 0): (1, 0), (2, 0): (2, 0), (3, 0): (2, 1),
-                 (0, 1): (3, 0), (1, 1): (3, 1), (2, 1): (4, 0), (3, 1): (4, 1)}
-        s_ps = {}
+        def entries(lst, j0, n):
+            return lst[:, j0 // 16 : (j0 + n) // 16]
+
+        xw_got = [sb.tile([P, HALF], U32, name=f"xw_got{h}", align_bytes=64) for h in range(2)]
         for h in range(2):
-            xw_got = sb.tile([P, HALF], U32, name=f"xw_got{h}", align_bytes=64)
-            nc.vector.tensor_copy(
-                xw_got[:], xw_win[:].bitcast(U32).indirect(offs_sb[:, h * HALF // 16 : (h + 1) * HALF // 16])
+            nc.vector.tensor_copy(xw_got[h][:], xw_win[:].bitcast(U32).indirect(entries(offs_sb, h * HALF, HALF)))
+        lead = sb.tile([P, HALF], F32, name="lead", align_bytes=64)
+        nc.vector.tensor_copy(lead[:], temp_win[0][:].indirect(entries(task_sb, 0, HALF)))
+
+        def score(dst, h, t):
+            nc.tensor.matmul_mx(
+                out=dst,
+                lhsT=dw_dealt[:, t * P : (t + 1) * P].bitcast(FP8X4),
+                lhsT_scale=planes[:, t * P : (t + 1) * P],
+                rhs=xw_got[h][:].bitcast(FP8X4),
+                rhs_scale=planes[:, H + h * HALF : H + (h + 1) * HALF],
+                start=True,
+                stop=True,
             )
-            for t in range(PACK):
-                b, e = place[t, h]
-                s_ps[t, h] = banks[b][:, e, :]
-                nc.tensor.matmul_mx(
-                    out=s_ps[t, h],
-                    lhsT=dw_dealt[:, t * P : (t + 1) * P].bitcast(FP8X4),
-                    lhsT_scale=planes[:, t * P : (t + 1) * P],
-                    rhs=xw_got[:].bitcast(FP8X4),
-                    rhs_scale=planes[:, H + h * HALF : H + (h + 1) * HALF],
-                    start=True,
-                    stop=True,
-                )
 
-        s_sb = [sb.tile([P, PACK, HALF], F32, name=f"s_sb{h}", tag=f"s_sb{h}", align_bytes=64) for h in range(2)]
-        y = {}
+        s_one = ps.tile([P, HALF], F32, name="s_one", tag="bank0")
+        s_lead = ps.tile([P, HALF], F32, name="s_lead", tag="bank1")
+        s_two = [ps.tile([P, 2, HALF], F32, name=f"s_two{b}", tag=f"bank{2 + b}") for b in range(3)]
+        s_sb = [sb.tile([P, PACK, HALF], F32, name=f"s_sb{h}", align_bytes=64) for h in range(2)]
+        score(s_one[:], 0, 1)
+        score(s_lead[:], 0, 0)
+        nc.scalar.copy(s_sb[0][:, 1, :], s_one[:])
+        for b, (h, t) in enumerate(((0, 2), (1, 0), (1, 2))):
+            score(s_two[b][:, 0, :], h, t)
+            score(s_two[b][:, 1, :], h, t + 1)
+            nc.scalar.copy(s_sb[h][:, t : t + 2, :], s_two[b][:])
 
-        def temper(t, h):
-            looked_up = temp_win[t][:].indirect(task_sb[:, h * HALF // 16 : (h + 1) * HALF // 16])
-            if (t, h) == (0, 0):
-                got = sb.tile([P, HALF], F32, name="tg", align_bytes=64)
-                nc.vector.tensor_copy(got[:], looked_up)
-                nc.vector.tensor_tensor(y[h][:, t, :], s_ps[t, h], got[:], MULT)
-            else:
-                nc.vector.tensor_tensor(y[h][:, t, :], looked_up, s_sb[h][:, t, :], MULT)
+        def temper(y, j0, n, t):
+            h, lo = divmod(j0, HALF)
+            looked_up = temp_win[t][:].indirect(entries(task_sb, j0, n))
+            nc.vector.tensor_tensor(y[:, t, lo : lo + n], looked_up, s_sb[h][:, t, lo : lo + n], MULT)
 
-        def squash(h, lo, n, label):
-            th = sb.tile([P, n, PACK], F32, name=f"th_{label}", align_bytes=64)
+        def squash(th, y):
             nc.scalar.activation(
-                th[:].rearrange("p (c i) t -> p c t i", i=4),
-                y[h][:, :, lo : lo + n].rearrange("p t (c i) -> p c t i", i=4),
+                th.rearrange("p (c i) t -> p c t i", i=4),
+                y.rearrange("p t (c i) -> p c t i", i=4),
                 ACT.Tanh,
                 scale=0.0625,
             )
-            return th
 
-        def weigh(z, th, n):
-            nc.vector.tensor_tensor(z, th[:], gn_sb[:].unsqueeze(1).to_broadcast([P, n, PACK]), MULT)
+        def weigh(z, th):
+            nc.vector.tensor_tensor(z, th, gn_sb[:].unsqueeze(1).to_broadcast(list(th.shape)), MULT)
 
-        def weave(copy, src, n, label):
-            woven = sb.tile([P, n, PACK], BF16, name=f"woven_{label}", tag=f"woven_{label}", align_bytes=64)
-            copy(woven[:].rearrange("p (c i) t -> p c t i", i=4), src.rearrange("p t (c i) -> p c t i", i=4))
-            return woven
+        def weave(woven, src):
+            nc.scalar.copy(woven.rearrange("p (c i) t -> p c t i", i=4), src.rearrange("p t (c i) -> p c t i", i=4))
 
-        def quantise(woven, n, label):
-            codes = sb.tile([P, n], U32, name=f"codes_{label}", align_bytes=64)
+        def quantise(woven, n, label, tag):
+            codes = sb.tile([P, n], U32, name=f"codes_{label}", tag=tag, align_bytes=64)
             scales = sb.tile([P, n], U8, name=f"scales_{label}", align_bytes=64)
             nc.vector.quantize_mx(
                 out=codes[:].bitcast(FP8X4), scales=scales[:], in_=woven[:].rearrange("p n t -> p (n t)")
@@ -158,53 +158,63 @@ def tile_picked_temper_tanh_p_kernel(
 
         out_rows = out.rearrange("(b p) j -> p b j", p=P)
 
-        def project(c, h, z_q, w_q, bank_tag, copy):
-            j0, n = CHUNKS[c]
-            res = sb.tile([P, 2, n], F32, name=f"res{c}{h}", align_bytes=64)
-            bank = ps.tile([P, 2, n], F32, name=f"o_bank{c}{h}", tag=bank_tag)
-            for e in range(2):
+        def project(res, j0, z_q, w_qs, b0, bank_tag, copy):
+            blocks, n = res.shape[1], res.shape[2]
+            bank = ps.tile([P, blocks, n], F32, name=f"o_bank{j0}_{b0}", tag=bank_tag)
+            for e in range(blocks):
+                w_q = w_qs[(b0 + e) // 2]
+                m0 = (b0 + e) % 2 * P
                 nc.tensor.matmul_mx(
                     out=bank[:, e, :],
-                    lhsT=w_q[0][:, e * P : (e + 1) * P].bitcast(FP8X4),
-                    lhsT_scale=w_q[1][:, e * P : (e + 1) * P],
+                    lhsT=w_q[0][:, m0 : m0 + P].bitcast(FP8X4),
+                    lhsT_scale=w_q[1][:, m0 : m0 + P],
                     rhs=z_q[0][:].bitcast(FP8X4),
                     rhs_scale=z_q[1][:],
                     start=True,
                     stop=True,
                 )
             copy(res[:], bank[:])
-            nc.sync.dma_start(out_rows[:, 2 * h : 2 * h + 2, j0 : j0 + n], res[:])
+            nc.sync.dma_start(out_rows[:, b0 : b0 + blocks, j0 : j0 + n], res[:])
 
+        def ring(tag, shape, dtype, name):
+            return sb.tile(shape, dtype, name=name, tag=tag, align_bytes=64)
+
+        ths = [P, CH, PACK]
         vcopy, scopy = nc.vector.tensor_copy, nc.scalar.copy
-        nc.scalar.copy(s_sb[0][:, 1, :], s_ps[1, 0])
-        nc.scalar.copy(s_sb[0][:, 2:4, :], banks[2][:])
-        nc.scalar.copy(s_sb[1][:, 0:2, :], banks[3][:])
-        nc.scalar.copy(s_sb[1][:, 2:4, :], banks[4][:])
-        y[0] = sb.tile([P, PACK, HALF], F32, name="y0", align_bytes=64)
+        ya = ring("ya", [P, PACK, HALF], F32, "ya")
+        nc.vector.tensor_tensor(ya[:, 0, :], s_lead[:], lead[:], MULT)
+        temper(ya, 0, HALF, 1)
+        for c in range(2):
+            for t in (2, 3):
+                temper(ya, c * CH, CH, t)
+        yb = ring("yb", [P, PACK, HALF], F32, "yb")
         for t in range(PACK):
-            temper(t, 0)
-        wa = weave(scopy, w_raw[0][:], HALF, "wa")
-        th0 = [squash(0, 128 * c, 128, f"0{c}") for c in range(2)]
-        y[1] = sb.tile([P, PACK, HALF], F32, name="y1", tag="s_sb0", align_bytes=64)
-        for t in range(PACK):
-            temper(t, 1)
-        wb = weave(scopy, w_raw[1][:], HALF, "wb")
-        th1 = [squash(1, 128 * c, 128, f"1{c}") for c in range(2)]
-        z0 = sb.tile([P, HALF, PACK], BF16, name="z0", align_bytes=64)
-        weigh(z0[:, 0:128, :], th0[0], 128)
-        weigh(z0[:, 128:256, :], th0[1], 128)
-        qwa = quantise(wa, HALF, "wa")
-        q0 = quantise(z0, HALF, "z0")
-        project(0, 0, q0, qwa, "bank5", scopy)
-        qwb = quantise(wb, HALF, "wb")
-        project(0, 1, q0, qwb, "bank6", scopy)
-        z1 = sb.tile([P, 128, PACK], BF16, name="z1", align_bytes=64)
-        z2 = sb.tile([P, 128, PACK], BF16, name="z2", align_bytes=64)
-        weigh(z1[:], th1[0], 128)
-        weigh(z2[:], th1[1], 128)
-        q1 = quantise(z1, 128, "z1")
-        project(1, 0, q1, qwa, "bank7", scopy)
-        project(1, 1, q1, qwb, "bank0", vcopy)
-        q2 = quantise(z2, 128, "z2")
-        project(2, 0, q2, qwa, "bank1", scopy)
-        project(2, 1, q2, qwb, "bank2", vcopy)
+            temper(yb, HALF, HALF, t)
+        th0 = ring("th0", ths, F32, "th0")
+        squash(th0[:], ya[:, :, 0:CH])
+        wa = ring("wa", [P, HALF, PACK], BF16, "wa")
+        weave(wa[:], w_raw[0][:])
+        th1 = shared.tile(ths, F32, name="th1", align_bytes=64, offset=6144)
+        squash(th1[:], ya[:, :, CH:HALF])
+        wb = ring("wb", [P, HALF, PACK], BF16, "wb")
+        weave(wb[:], w_raw[1][:])
+        th2 = ring("dw_got", [P, HALF, PACK], F32, "th2")
+        squash(th2[:, 0:CH, :], yb[:, :, 0:CH])
+        squash(th2[:, CH:HALF, :], yb[:, :, CH:HALF])
+        z01 = ring("z01", [P, HALF, PACK], BF16, "z01")
+        weigh(z01[:, 0:CH, :], th0[:])
+        weigh(z01[:, CH:HALF, :], th1[:])
+        qw = [quantise(wa, HALF, "wa", "ya")]
+        q01 = quantise(z01, HALF, "z01", "codes_z01")
+        z2 = ring("z2", ths, BF16, "z2")
+        weigh(z2[:], th2[:, 0:CH, :])
+        qw.append(quantise(wb, HALF, "wb", "codes_wb"))
+        q2 = quantise(z2, CH, "z2", "codes_z2")
+        z3 = ring("z3", ths, BF16, "z3")
+        weigh(z3[:], th2[:, CH:HALF, :])
+        q3 = quantise(z3, CH, "z3", "codes_z3")
+        project(ring("yb", [P, 2, HALF], F32, "res_a"), 0, q01, qw, 0, "bank5", scopy)
+        project(ring("res_b", [P, 2, HALF], F32, "res_b"), 0, q01, qw, 2, "bank6", scopy)
+        project(ring("res_2", [P, 4, CH], F32, "res_2"), 2 * CH, q2, qw, 0, "bank7", scopy)
+        project(ring("res_3a", [P, 2, CH], F32, "res_3a"), 3 * CH, q3, qw, 0, "bank0", scopy)
+        project(ring("res_3b", [P, 2, CH], F32, "res_3b"), 3 * CH, q3, qw, 2, "bank1", vcopy)

@@ -67,12 +67,23 @@ def tile_picked_temper_tanh_p_kernel(
         dsc_got = sb.tile([P, H], U8, name="dsc_got", align_bytes=64)
         xsc_got = shared.tile([P, S], U8, name="xsc_got", align_bytes=64, offset=1792)
         planes = sb.tile([P, H + S], U8, name="planes", align_bytes=64)
-        nc.vector.tensor_copy(dsc_got[:], dsc_win[:].indirect(kidx_sb[:]))
+
+        def entries(lst, j0, n):
+            return lst[:, j0 // 16 : (j0 + n) // 16]
+
+        def deal(dealt, got, h):
+            nc.vector.tensor_copy(
+                dealt.rearrange("p (t m) -> p m t", t=PACK)[:, h * 64 : (h + 1) * 64, :],
+                got[:, h * HALF : (h + 1) * HALF].rearrange("p (m t) -> p m t", t=PACK),
+            )
+
+        for h in range(2):
+            nc.vector.tensor_copy(
+                dsc_got[:, h * HALF : (h + 1) * HALF], dsc_win[:].indirect(entries(kidx_sb, h * HALF, HALF))
+            )
+        deal(planes[:, 0:H], dsc_got, 0)
         nc.vector.tensor_copy(xsc_got[:], xsc_win[:].indirect(offs_sb[:]))
-        nc.vector.tensor_copy(
-            planes[:, 0:H].rearrange("p (t m) -> p m t", t=PACK),
-            dsc_got[:].rearrange("p (m t) -> p m t", t=PACK),
-        )
+        deal(planes[:, 0:H], dsc_got, 1)
         nc.vector.tensor_copy(planes[:, H : H + S].bitcast(I32), xsc_got[:].bitcast(I32))
         for r in range(1, PACK):
             nc.sync.dma_start(planes[r:P:32, :].bitcast(I32), planes[8 * r : P : 32, :].bitcast(I32))
@@ -80,15 +91,17 @@ def tile_picked_temper_tanh_p_kernel(
         temp_win.append(load_temp(2, 2048))
 
         dw_got = sb.tile([P, H], U32, name="dw_got", tag="dw_got", align_bytes=64)
-        dw_dealt = sb.tile([P, H], U32, name="dw_dealt", align_bytes=64)
-        nc.vector.tensor_copy(dw_got[:], dw_win[:].bitcast(U32).indirect(kidx_sb[:]))
-        nc.vector.tensor_copy(
-            dw_dealt[:].rearrange("p (t m) -> p m t", t=PACK),
-            dw_got[:].rearrange("p (m t) -> p m t", t=PACK),
-        )
+        dw_dealt = sb.tile([P, H], U32, name="dw_dealt", tag="dw_dealt", align_bytes=64)
+        for h in range(2):
+            nc.vector.tensor_copy(
+                dw_got[:, h * HALF : (h + 1) * HALF],
+                dw_win[:].bitcast(U32).indirect(entries(kidx_sb, h * HALF, HALF)),
+            )
+        for h in range(2):
+            deal(dw_dealt[:], dw_got, h)
         temp_win.append(load_temp(3, 4096))
-        gn_sb = shared.tile([P, PACK], F32, name="gn_sb", align_bytes=64, offset=10240)
-        nc.sync.dma_start(gn_sb[:], gn.rearrange("(p t) o -> p (t o)", t=PACK))
+        gn_sb = sb.tile([P, PACK], F32, name="gn_sb")
+        nc.gpsimd.dma_start(gn_sb[:], gn[:, 0].rearrange("(p t) -> p t", t=PACK))
         w_rows = w1.rearrange("(p t) m -> p t m", t=PACK)
         w_raw = [
             shared.tile([P, PACK, HALF], F32, name="w_raw0", align_bytes=64, offset=6144),
@@ -97,12 +110,11 @@ def tile_picked_temper_tanh_p_kernel(
         for h in range(2):
             nc.sync.dma_start(w_raw[h][:], w_rows[:, :, h * HALF : (h + 1) * HALF])
 
-        def entries(lst, j0, n):
-            return lst[:, j0 // 16 : (j0 + n) // 16]
-
-        xw_got = [sb.tile([P, HALF], U32, name=f"xw_got{h}", align_bytes=64) for h in range(2)]
+        xw_got = sb.tile([P, S], U32, name="xw_got", align_bytes=64)
         for h in range(2):
-            nc.vector.tensor_copy(xw_got[h][:], xw_win[:].bitcast(U32).indirect(entries(offs_sb, h * HALF, HALF)))
+            nc.vector.tensor_copy(
+                xw_got[:, h * HALF : (h + 1) * HALF], xw_win[:].bitcast(U32).indirect(entries(offs_sb, h * HALF, HALF))
+            )
         lead = sb.tile([P, HALF], F32, name="lead", align_bytes=64)
         nc.vector.tensor_copy(lead[:], temp_win[0][:].indirect(entries(task_sb, 0, HALF)))
 
@@ -111,28 +123,25 @@ def tile_picked_temper_tanh_p_kernel(
                 out=dst,
                 lhsT=dw_dealt[:, t * P : (t + 1) * P].bitcast(FP8X4),
                 lhsT_scale=planes[:, t * P : (t + 1) * P],
-                rhs=xw_got[h][:].bitcast(FP8X4),
+                rhs=xw_got[:, h * HALF : (h + 1) * HALF].bitcast(FP8X4),
                 rhs_scale=planes[:, H + h * HALF : H + (h + 1) * HALF],
                 start=True,
                 stop=True,
             )
 
-        s_one = ps.tile([P, HALF], F32, name="s_one", tag="bank0")
-        s_lead = ps.tile([P, HALF], F32, name="s_lead", tag="bank1")
-        s_two = [ps.tile([P, 2, HALF], F32, name=f"s_two{b}", tag=f"bank{2 + b}") for b in range(3)]
-        s_sb = [sb.tile([P, PACK, HALF], F32, name=f"s_sb{h}", align_bytes=64) for h in range(2)]
-        score(s_one[:], 0, 1)
+        s_sb = [sb.tile([P, PACK, HALF], F32, name=f"s_sb{h}", tag=f"s_sb{h}", align_bytes=64) for h in range(2)]
+        s_lead = ps.tile([P, HALF], F32, name="s_lead", tag="bank0")
         score(s_lead[:], 0, 0)
-        nc.scalar.copy(s_sb[0][:, 1, :], s_one[:])
-        for b, (h, t) in enumerate(((0, 2), (1, 0), (1, 2))):
-            score(s_two[b][:, 0, :], h, t)
-            score(s_two[b][:, 1, :], h, t + 1)
-            nc.scalar.copy(s_sb[h][:, t : t + 2, :], s_two[b][:])
+        for b, (h, t0, slots) in enumerate(((0, 1, 1), (0, 2, 2), (1, 0, 2), (1, 2, 2))):
+            bank = ps.tile([P, slots, HALF], F32, name=f"s_bank{b}", tag=f"bank{b + 1}")
+            for e in range(slots):
+                score(bank[:, e, :], h, t0 + e)
+            nc.scalar.copy(s_sb[h][:, t0 : t0 + slots, :], bank[:])
 
-        def temper(y, j0, n, t):
-            h, lo = divmod(j0, HALF)
-            looked_up = temp_win[t][:].indirect(entries(task_sb, j0, n))
-            nc.vector.tensor_tensor(y[:, t, lo : lo + n], looked_up, s_sb[h][:, t, lo : lo + n], MULT)
+        def temper(y, h):
+            for t in range(1 - h, PACK):
+                looked_up = temp_win[t][:].indirect(entries(task_sb, h * HALF, HALF))
+                nc.vector.tensor_tensor(y[:, t, :], looked_up, s_sb[h][:, t, :], MULT)
 
         def squash(th, y):
             nc.scalar.activation(
@@ -148,12 +157,11 @@ def tile_picked_temper_tanh_p_kernel(
         def weave(woven, src):
             nc.scalar.copy(woven.rearrange("p (c i) t -> p c t i", i=4), src.rearrange("p t (c i) -> p c t i", i=4))
 
-        def quantise(woven, n, label, tag):
-            codes = sb.tile([P, n], U32, name=f"codes_{label}", tag=tag, align_bytes=64)
+        def quantise(woven, label, offset):
+            n = woven.shape[1]
+            codes = shared.tile([P, n], U32, name=f"codes_{label}", align_bytes=64, offset=offset)
             scales = sb.tile([P, n], U8, name=f"scales_{label}", align_bytes=64)
-            nc.vector.quantize_mx(
-                out=codes[:].bitcast(FP8X4), scales=scales[:], in_=woven[:].rearrange("p n t -> p (n t)")
-            )
+            nc.vector.quantize_mx(out=codes[:].bitcast(FP8X4), scales=scales[:], in_=woven.rearrange("p n t -> p (n t)"))
             return codes, scales
 
         out_rows = out.rearrange("(b p) j -> p b j", p=P)
@@ -162,8 +170,7 @@ def tile_picked_temper_tanh_p_kernel(
             blocks, n = res.shape[1], res.shape[2]
             bank = ps.tile([P, blocks, n], F32, name=f"o_bank{j0}_{b0}", tag=bank_tag)
             for e in range(blocks):
-                w_q = w_qs[(b0 + e) // 2]
-                m0 = (b0 + e) % 2 * P
+                w_q, m0 = w_qs[b0 + e]
                 nc.tensor.matmul_mx(
                     out=bank[:, e, :],
                     lhsT=w_q[0][:, m0 : m0 + P].bitcast(FP8X4),
@@ -181,39 +188,46 @@ def tile_picked_temper_tanh_p_kernel(
 
         ths = [P, CH, PACK]
         vcopy, scopy = nc.vector.tensor_copy, nc.scalar.copy
-        ya = ring("ya", [P, PACK, HALF], F32, "ya")
+        ya = shared.tile([P, PACK, HALF], F32, name="ya", align_bytes=64, offset=20480)
         nc.vector.tensor_tensor(ya[:, 0, :], s_lead[:], lead[:], MULT)
-        temper(ya, 0, HALF, 1)
-        for c in range(2):
-            for t in (2, 3):
-                temper(ya, c * CH, CH, t)
+        temper(ya, 0)
         yb = ring("yb", [P, PACK, HALF], F32, "yb")
-        for t in range(PACK):
-            temper(yb, HALF, HALF, t)
-        th0 = ring("th0", ths, F32, "th0")
-        squash(th0[:], ya[:, :, 0:CH])
+        temper(yb, 1)
         wa = ring("wa", [P, HALF, PACK], BF16, "wa")
         weave(wa[:], w_raw[0][:])
-        th1 = shared.tile(ths, F32, name="th1", align_bytes=64, offset=6144)
-        squash(th1[:], ya[:, :, CH:HALF])
-        wb = ring("wb", [P, HALF, PACK], BF16, "wb")
+        th01 = shared.tile([P, HALF, PACK], F32, name="th01", align_bytes=64, offset=6144 + 2048)
+        squash(th01[:], ya[:])
+        wb = shared.tile([P, HALF, PACK], BF16, name="wb", align_bytes=64, offset=6144)
         weave(wb[:], w_raw[1][:])
-        th2 = ring("dw_got", [P, HALF, PACK], F32, "th2")
-        squash(th2[:, 0:CH, :], yb[:, :, 0:CH])
-        squash(th2[:, CH:HALF, :], yb[:, :, CH:HALF])
+        th2 = shared.tile(ths, F32, name="th2", align_bytes=64, offset=20480 + 1024)
+        squash(th2[:], yb[:, :, 0:CH])
+        th3 = shared.tile(ths, F32, name="th3", align_bytes=64, offset=24576 - 512)
+        squash(th3[:], yb[:, :, CH:HALF])
+        qa0 = quantise(wa[:, 0:CH, :], "wa0", 16384)
+        for e in range(2):
+            idle = ps.tile([P, S], F32, name=f"idle{e}", tag=f"bank{3 + e}")
+            nc.tensor.matmul_mx(
+                out=idle[:],
+                lhsT=qa0[0][:].bitcast(FP8X4),
+                lhsT_scale=qa0[1][:],
+                rhs=xw_got[:].bitcast(FP8X4),
+                rhs_scale=planes[:, H : H + S],
+                start=True,
+                stop=True,
+            )
         z01 = ring("z01", [P, HALF, PACK], BF16, "z01")
-        weigh(z01[:, 0:CH, :], th0[:])
-        weigh(z01[:, CH:HALF, :], th1[:])
-        qw = [quantise(wa, HALF, "wa", "ya")]
-        q01 = quantise(z01, HALF, "z01", "codes_z01")
+        weigh(z01[:], th01[:])
+        qa1 = quantise(wa[:, CH:HALF, :], "wa1", 20480)
+        q01 = quantise(z01[:], "z01", 17408)
+        qb = quantise(wb[:], "wb", 18432)
+        qw = [(qa0, 0), (qa1, 0), (qb, 0), (qb, P)]
         z2 = ring("z2", ths, BF16, "z2")
-        weigh(z2[:], th2[:, 0:CH, :])
-        qw.append(quantise(wb, HALF, "wb", "codes_wb"))
-        q2 = quantise(z2, CH, "z2", "codes_z2")
-        z3 = ring("z3", ths, BF16, "z3")
-        weigh(z3[:], th2[:, CH:HALF, :])
-        q3 = quantise(z3, CH, "z3", "codes_z3")
-        project(ring("yb", [P, 2, HALF], F32, "res_a"), 0, q01, qw, 0, "bank5", scopy)
+        weigh(z2[:], th2[:])
+        q2 = quantise(z2[:], "z2", 19456)
+        z3 = shared.tile(ths, BF16, name="z3", align_bytes=64, offset=20480 + 1024)
+        weigh(z3[:], th3[:])
+        q3 = quantise(z3[:], "z3", 19968)
+        project(ring("res_a", [P, 2, HALF], F32, "res_a"), 0, q01, qw, 0, "bank5", scopy)
         project(ring("res_b", [P, 2, HALF], F32, "res_b"), 0, q01, qw, 2, "bank6", scopy)
         project(ring("res_2", [P, 4, CH], F32, "res_2"), 2 * CH, q2, qw, 0, "bank7", scopy)
         project(ring("res_3a", [P, 2, CH], F32, "res_3a"), 3 * CH, q3, qw, 0, "bank0", scopy)

@@ -100,8 +100,6 @@ def tile_picked_temper_tanh_p_kernel(
         for h in range(2):
             deal(dw_dealt[:], dw_got, h)
         temp_win.append(load_temp(3, 4096))
-        gn_sb = sb.tile([P, PACK], F32, name="gn_sb")
-        nc.gpsimd.dma_start(gn_sb[:], gn[:, 0].rearrange("(p t) -> p t", t=PACK))
         w_rows = w1.rearrange("(p t) m -> p t m", t=PACK)
         w_raw = [
             shared.tile([P, PACK, HALF], F32, name="w_raw0", align_bytes=64, offset=6144),
@@ -115,6 +113,8 @@ def tile_picked_temper_tanh_p_kernel(
             nc.vector.tensor_copy(
                 xw_got[:, h * HALF : (h + 1) * HALF], xw_win[:].bitcast(U32).indirect(entries(offs_sb, h * HALF, HALF))
             )
+        gn_sb = sb.tile([P, PACK], F32, name="gn_sb", tag="xw_win", align_bytes=64)
+        nc.sync.dma_start(gn_sb[:], gn[:, 0].rearrange("(p t) -> p t", t=PACK))
         lead = sb.tile([P, HALF], F32, name="lead", align_bytes=64)
         nc.vector.tensor_copy(lead[:], temp_win[0][:].indirect(entries(task_sb, 0, HALF)))
 

@@ -183,6 +183,25 @@ def tile_picked_temper_tanh_p_kernel(
             copy(res[:], bank[:])
             nc.sync.dma_start(out_rows[:, b0 : b0 + blocks, j0 : j0 + n], res[:])
 
+        def project_last(j0, z_q, w_qs, banks):
+            for pair in range(2):
+                res = sb.tile([P, 2, CH], F32, name=f"res_last{pair}", align_bytes=64)
+                for e, copy in enumerate((nc.scalar.copy, nc.vector.tensor_copy)):
+                    block = 2 * pair + e
+                    bank = ps.tile([P, CH], F32, name=f"o_last{block}", tag=banks[block])
+                    w_q, m0 = w_qs[block]
+                    nc.tensor.matmul_mx(
+                        out=bank[:],
+                        lhsT=w_q[0][:, m0 : m0 + P].bitcast(FP8X4),
+                        lhsT_scale=w_q[1][:, m0 : m0 + P],
+                        rhs=z_q[0][:].bitcast(FP8X4),
+                        rhs_scale=z_q[1][:],
+                        start=True,
+                        stop=True,
+                    )
+                    copy(res[:, e, :], bank[:])
+                nc.sync.dma_start(out_rows[:, 2 * pair : 2 * pair + 2, j0 : j0 + CH], res[:])
+
         def ring(tag, shape, dtype, name):
             return sb.tile(shape, dtype, name=name, tag=tag, align_bytes=64)
 
@@ -227,8 +246,8 @@ def tile_picked_temper_tanh_p_kernel(
         z3 = shared.tile(ths, BF16, name="z3", align_bytes=64, offset=20480 + 1024)
         weigh(z3[:], th3[:])
         q3 = quantise(z3[:], "z3", 19968)
-        project(ring("res_a", [P, 2, HALF], F32, "res_a"), 0, q01, qw, 0, "bank5", scopy)
-        project(ring("res_b", [P, 2, HALF], F32, "res_b"), 0, q01, qw, 2, "bank6", scopy)
-        project(ring("res_2", [P, 4, CH], F32, "res_2"), 2 * CH, q2, qw, 0, "bank7", scopy)
-        project(ring("res_3a", [P, 2, CH], F32, "res_3a"), 3 * CH, q3, qw, 0, "bank0", scopy)
-        project(ring("res_3b", [P, 2, CH], F32, "res_3b"), 3 * CH, q3, qw, 2, "bank1", vcopy)
+        project(ring("res_a0", [P, 1, HALF], F32, "res_a0"), 0, q01, qw, 0, "bank5", scopy)
+        project(ring("res_a1", [P, 1, HALF], F32, "res_a1"), 0, q01, qw, 1, "bank6", scopy)
+        project(ring("res_b", [P, 2, HALF], F32, "res_b"), 0, q01, qw, 2, "bank7", scopy)
+        project(ring("res_2", [P, 4, CH], F32, "res_2"), 2 * CH, q2, qw, 0, "bank4", scopy)
+        project_last(3 * CH, q3, qw, ("bank0", "bank1", "bank2", "bank3"))

@@ -183,25 +183,6 @@ def tile_picked_temper_tanh_p_kernel(
             copy(res[:], bank[:])
             nc.sync.dma_start(out_rows[:, b0 : b0 + blocks, j0 : j0 + n], res[:])
 
-        def project_last(j0, z_q, w_qs, banks):
-            for pair in range(2):
-                res = sb.tile([P, 2, CH], F32, name=f"res_last{pair}", align_bytes=64)
-                for e, copy in enumerate((nc.scalar.copy, nc.vector.tensor_copy)):
-                    block = 2 * pair + e
-                    bank = ps.tile([P, CH], F32, name=f"o_last{block}", tag=banks[block])
-                    w_q, m0 = w_qs[block]
-                    nc.tensor.matmul_mx(
-                        out=bank[:],
-                        lhsT=w_q[0][:, m0 : m0 + P].bitcast(FP8X4),
-                        lhsT_scale=w_q[1][:, m0 : m0 + P],
-                        rhs=z_q[0][:].bitcast(FP8X4),
-                        rhs_scale=z_q[1][:],
-                        start=True,
-                        stop=True,
-                    )
-                    copy(res[:, e, :], bank[:])
-                nc.sync.dma_start(out_rows[:, 2 * pair : 2 * pair + 2, j0 : j0 + CH], res[:])
-
         def ring(tag, shape, dtype, name):
             return sb.tile(shape, dtype, name=name, tag=tag, align_bytes=64)
 
@@ -210,7 +191,7 @@ def tile_picked_temper_tanh_p_kernel(
         ya = shared.tile([P, PACK, HALF], F32, name="ya", align_bytes=64, offset=20480)
         nc.vector.tensor_tensor(ya[:, 0, :], s_lead[:], lead[:], MULT)
         temper(ya, 0)
-        yb = ring("yb", [P, PACK, HALF], F32, "yb")
+        yb = shared.tile([P, PACK, HALF], F32, name="yb", align_bytes=64, offset=28672)
         temper(yb, 1)
         wa = ring("wa", [P, HALF, PACK], BF16, "wa")
         weave(wa[:], w_raw[0][:])
@@ -222,13 +203,13 @@ def tile_picked_temper_tanh_p_kernel(
         squash(th2[:], yb[:, :, 0:CH])
         th3 = shared.tile(ths, F32, name="th3", align_bytes=64, offset=24576 - 512)
         squash(th3[:], yb[:, :, CH:HALF])
-        qa0 = quantise(wa[:, 0:CH, :], "wa0", 16384)
+        qa = quantise(wa[:], "wa", 16384)
         for e in range(2):
             idle = ps.tile([P, S], F32, name=f"idle{e}", tag=f"bank{3 + e}")
             nc.tensor.matmul_mx(
                 out=idle[:],
-                lhsT=qa0[0][:].bitcast(FP8X4),
-                lhsT_scale=qa0[1][:],
+                lhsT=qa[0][:, 0:P].bitcast(FP8X4),
+                lhsT_scale=qa[1][:, 0:P],
                 rhs=xw_got[:].bitcast(FP8X4),
                 rhs_scale=planes[:, H : H + S],
                 start=True,
@@ -236,18 +217,18 @@ def tile_picked_temper_tanh_p_kernel(
             )
         z01 = ring("z01", [P, HALF, PACK], BF16, "z01")
         weigh(z01[:], th01[:])
-        qa1 = quantise(wa[:, CH:HALF, :], "wa1", 20480)
-        q01 = quantise(z01[:], "z01", 17408)
         qb = quantise(wb[:], "wb", 18432)
-        qw = [(qa0, 0), (qa1, 0), (qb, 0), (qb, P)]
+        q01 = quantise(z01[:], "z01", 17408)
+        qw = [(qa, 0), (qa, P), (qb, 0), (qb, P)]
         z2 = ring("z2", ths, BF16, "z2")
         weigh(z2[:], th2[:])
-        q2 = quantise(z2[:], "z2", 19456)
-        z3 = shared.tile(ths, BF16, name="z3", align_bytes=64, offset=20480 + 1024)
+        z3 = ring("z3", ths, BF16, "z3")
         weigh(z3[:], th3[:])
+        q2 = quantise(z2[:], "z2", 28672)
         q3 = quantise(z3[:], "z3", 19968)
-        project(ring("res_a0", [P, 1, HALF], F32, "res_a0"), 0, q01, qw, 0, "bank5", scopy)
-        project(ring("res_a1", [P, 1, HALF], F32, "res_a1"), 0, q01, qw, 1, "bank6", scopy)
-        project(ring("res_b", [P, 2, HALF], F32, "res_b"), 0, q01, qw, 2, "bank7", scopy)
-        project(ring("res_2", [P, 4, CH], F32, "res_2"), 2 * CH, q2, qw, 0, "bank4", scopy)
-        project_last(3 * CH, q3, qw, ("bank0", "bank1", "bank2", "bank3"))
+        for block, bank in enumerate(("bank5", "bank6", "bank7", "bank0")):
+            project(ring(f"res_a{block}", [P, 1, HALF], F32, f"res_a{block}"), 0, q01, qw, block, bank, scopy)
+        project(ring("res_2a", [P, 2, CH], F32, "res_2a"), 2 * CH, q2, qw, 0, "bank1", scopy)
+        project(ring("res_2b", [P, 2, CH], F32, "res_2b"), 2 * CH, q2, qw, 2, "bank2", vcopy)
+        project(ring("res_3a", [P, 2, CH], F32, "res_3a"), 3 * CH, q3, qw, 0, "bank3", scopy)
+        project(ring("res_3b", [P, 2, CH], F32, "res_3b"), 3 * CH, q3, qw, 2, "bank4", vcopy)

@@ -45,9 +45,6 @@ def tile_picked_temper_tanh_p_kernel(
         nc.sync.dma_start(dsc_win[:].bitcast(I32), d_scales[0].bitcast(I32).unsqueeze(1).to_broadcast(spread))
         nc.sync.dma_start(offs_sb[:], offs)
         nc.sync.dma_start(xsc_win[0:P:8, :].bitcast(I32), x_scales[0].bitcast(I32))
-        warm = sb.tile([P, 2], F32, name="warm")
-        nc.vector.memset(warm[:, 0:1], 0.0)
-        nc.scalar.activation(warm[:, 1:2], warm[:, 0:1], ACT.Tanh)
 
         dw_win = shared.tile([P, TABLE], I32, name="dw_win", align_bytes=64, offset=4096)
         xw_win = sb.tile([P, TABLE], I32, name="xw_win", align_bytes=64)
@@ -66,24 +63,20 @@ def tile_picked_temper_tanh_p_kernel(
 
         dsc_got = sb.tile([P, H], U8, name="dsc_got", align_bytes=64)
         xsc_got = shared.tile([P, S], U8, name="xsc_got", align_bytes=64, offset=1792)
-        planes = sb.tile([P, H + S], U8, name="planes", align_bytes=64)
 
         def entries(lst, j0, n):
             return lst[:, j0 // 16 : (j0 + n) // 16]
 
-        def deal(dealt, got, h):
+        def deal(dealt, got, key0, keys):
             nc.vector.tensor_copy(
-                dealt.rearrange("p (t m) -> p m t", t=PACK)[:, h * 64 : (h + 1) * 64, :],
-                got[:, h * HALF : (h + 1) * HALF].rearrange("p (m t) -> p m t", t=PACK),
+                dealt.rearrange("p (t m) -> p m t", t=PACK)[:, key0 // PACK : (key0 + keys) // PACK, :],
+                got[:, key0 : key0 + keys].rearrange("p (m t) -> p m t", t=PACK),
             )
 
-        for h in range(2):
-            nc.vector.tensor_copy(
-                dsc_got[:, h * HALF : (h + 1) * HALF], dsc_win[:].indirect(entries(kidx_sb, h * HALF, HALF))
-            )
-        deal(planes[:, 0:H], dsc_got, 0)
+        nc.vector.tensor_copy(dsc_got[:], dsc_win[:].indirect(kidx_sb[:]))
         nc.vector.tensor_copy(xsc_got[:], xsc_win[:].indirect(offs_sb[:]))
-        deal(planes[:, 0:H], dsc_got, 1)
+        planes = sb.tile([P, H + S], U8, name="planes", tag="xsc_win", align_bytes=64)
+        deal(planes[:, 0:H], dsc_got, 0, H)
         nc.vector.tensor_copy(planes[:, H : H + S].bitcast(I32), xsc_got[:].bitcast(I32))
         for r in range(1, PACK):
             nc.sync.dma_start(planes[r:P:32, :].bitcast(I32), planes[8 * r : P : 32, :].bitcast(I32))
@@ -98,7 +91,7 @@ def tile_picked_temper_tanh_p_kernel(
                 dw_win[:].bitcast(U32).indirect(entries(kidx_sb, h * HALF, HALF)),
             )
         for h in range(2):
-            deal(dw_dealt[:], dw_got, h)
+            deal(dw_dealt[:], dw_got, h * HALF, HALF)
         temp_win.append(load_temp(3, 4096))
         w_rows = w1.rearrange("(p t) m -> p t m", t=PACK)
         w_raw = [
@@ -115,8 +108,6 @@ def tile_picked_temper_tanh_p_kernel(
             )
         gn_sb = sb.tile([P, PACK], F32, name="gn_sb", tag="xw_win", align_bytes=64)
         nc.sync.dma_start(gn_sb[:], gn[:, 0].rearrange("(p t) -> p t", t=PACK))
-        lead = sb.tile([P, HALF], F32, name="lead", align_bytes=64)
-        nc.vector.tensor_copy(lead[:], temp_win[0][:].indirect(entries(task_sb, 0, HALF)))
 
         def score(dst, h, t):
             nc.tensor.matmul_mx(
@@ -130,16 +121,14 @@ def tile_picked_temper_tanh_p_kernel(
             )
 
         s_sb = [sb.tile([P, PACK, HALF], F32, name=f"s_sb{h}", tag=f"s_sb{h}", align_bytes=64) for h in range(2)]
-        s_lead = ps.tile([P, HALF], F32, name="s_lead", tag="bank0")
-        score(s_lead[:], 0, 0)
-        for b, (h, t0, slots) in enumerate(((0, 1, 1), (0, 2, 2), (1, 0, 2), (1, 2, 2))):
-            bank = ps.tile([P, slots, HALF], F32, name=f"s_bank{b}", tag=f"bank{b + 1}")
+        for b, (h, t0, slots) in enumerate(((0, 0, 1), (0, 1, 1), (0, 2, 2), (1, 0, 2), (1, 2, 2))):
+            bank = ps.tile([P, slots, HALF], F32, name=f"s_bank{b}", tag=f"bank{b}")
             for e in range(slots):
                 score(bank[:, e, :], h, t0 + e)
             nc.scalar.copy(s_sb[h][:, t0 : t0 + slots, :], bank[:])
 
         def temper(y, h):
-            for t in range(1 - h, PACK):
+            for t in range(PACK):
                 looked_up = temp_win[t][:].indirect(entries(task_sb, h * HALF, HALF))
                 nc.vector.tensor_tensor(y[:, t, :], looked_up, s_sb[h][:, t, :], MULT)
 
@@ -189,7 +178,6 @@ def tile_picked_temper_tanh_p_kernel(
         ths = [P, CH, PACK]
         vcopy, scopy = nc.vector.tensor_copy, nc.scalar.copy
         ya = shared.tile([P, PACK, HALF], F32, name="ya", align_bytes=64, offset=20480)
-        nc.vector.tensor_tensor(ya[:, 0, :], s_lead[:], lead[:], MULT)
         temper(ya, 0)
         yb = shared.tile([P, PACK, HALF], F32, name="yb", align_bytes=64, offset=28672)
         temper(yb, 1)

@@ -192,17 +192,6 @@ def tile_picked_temper_tanh_p_kernel(
         th3 = shared.tile(ths, F32, name="th3", align_bytes=64, offset=24576 - 512)
         squash(th3[:], yb[:, :, CH:HALF])
         qa = quantise(wa[:], "wa", 16384)
-        for e in range(2):
-            idle = ps.tile([P, S], F32, name=f"idle{e}", tag=f"bank{3 + e}")
-            nc.tensor.matmul_mx(
-                out=idle[:],
-                lhsT=qa[0][:, 0:P].bitcast(FP8X4),
-                lhsT_scale=qa[1][:, 0:P],
-                rhs=xw_got[:].bitcast(FP8X4),
-                rhs_scale=planes[:, H : H + S],
-                start=True,
-                stop=True,
-            )
         z01 = ring("z01", [P, HALF, PACK], BF16, "z01")
         weigh(z01[:], th01[:])
         qb = quantise(wb[:], "wb", 18432)

@@ -45,13 +45,13 @@ def tile_picked_temper_tanh_p_kernel(
         nc.sync.dma_start(dsc_win[:].bitcast(I32), d_scales[0].bitcast(I32).unsqueeze(1).to_broadcast(spread))
         nc.sync.dma_start(offs_sb[:], offs)
         nc.sync.dma_start(xsc_win[0:P:8, :].bitcast(I32), x_scales[0].bitcast(I32))
+        nc.sync.dma_start(task_sb[:], task)
 
-        dw_win = shared.tile([P, TABLE], I32, name="dw_win", align_bytes=64, offset=4096)
+        dw_win = shared.tile([P, TABLE], I32, name="dw_win", align_bytes=64, offset=6144)
         xw_win = sb.tile([P, TABLE], I32, name="xw_win", align_bytes=64)
         nc.sync.dma_start(dw_win[:], d_words[0].rearrange("p n t -> p (n t)").bitcast(I32))
         nc.sync.dma_start(xw_win[:], x_words[0].rearrange("p n t -> p (n t)").bitcast(I32))
 
-        nc.sync.dma_start(task_sb[:], task)
         temp_rows = temp.rearrange("(p t) u -> p t u", t=PACK)
 
         def load_temp(t, offset):
@@ -59,7 +59,7 @@ def tile_picked_temper_tanh_p_kernel(
             nc.sync.dma_start(win[:], temp_rows[:, t, :])
             return win
 
-        temp_win = [load_temp(0, 12288)]
+        temp_win = [load_temp(0, 14336)]
 
         dsc_got = sb.tile([P, H], U8, name="dsc_got", align_bytes=64)
         xsc_got = shared.tile([P, S], U8, name="xsc_got", align_bytes=64, offset=1792)
@@ -81,10 +81,15 @@ def tile_picked_temper_tanh_p_kernel(
         for r in range(1, PACK):
             nc.sync.dma_start(planes[r:P:32, :].bitcast(I32), planes[8 * r : P : 32, :].bitcast(I32))
         temp_win.append(load_temp(1, 0))
-        temp_win.append(load_temp(2, 2048))
+        w_rows = w1.rearrange("(p t) m -> p t m", t=PACK)
+        w_raw = [
+            shared.tile([P, PACK, HALF], F32, name="w_raw0", align_bytes=64, offset=2048),
+            sb.tile([P, PACK, HALF], F32, name="w_raw1", tag="dw_got", align_bytes=64),
+        ]
+        nc.sync.dma_start(w_raw[0][:], w_rows[:, :, 0:HALF])
 
         dw_got = sb.tile([P, H], U32, name="dw_got", tag="dw_got", align_bytes=64)
-        dw_dealt = sb.tile([P, H], U32, name="dw_dealt", tag="dw_dealt", align_bytes=64)
+        dw_dealt = shared.tile([P, H], U32, name="dw_dealt", align_bytes=64, offset=16384)
         for h in range(2):
             nc.vector.tensor_copy(
                 dw_got[:, h * HALF : (h + 1) * HALF],
@@ -92,16 +97,11 @@ def tile_picked_temper_tanh_p_kernel(
             )
         for h in range(2):
             deal(dw_dealt[:], dw_got, h * HALF, HALF)
-        temp_win.append(load_temp(3, 4096))
-        w_rows = w1.rearrange("(p t) m -> p t m", t=PACK)
-        w_raw = [
-            shared.tile([P, PACK, HALF], F32, name="w_raw0", align_bytes=64, offset=6144),
-            sb.tile([P, PACK, HALF], F32, name="w_raw1", tag="dw_got", align_bytes=64),
-        ]
-        for h in range(2):
-            nc.sync.dma_start(w_raw[h][:], w_rows[:, :, h * HALF : (h + 1) * HALF])
+        temp_win.append(load_temp(2, 6144))
+        temp_win.append(load_temp(3, 8192))
+        nc.sync.dma_start(w_raw[1][:], w_rows[:, :, HALF:N])
 
-        xw_got = sb.tile([P, S], U32, name="xw_got", align_bytes=64)
+        xw_got = sb.tile([P, S], U32, name="xw_got", tag="xw_got", align_bytes=64)
         for h in range(2):
             nc.vector.tensor_copy(
                 xw_got[:, h * HALF : (h + 1) * HALF], xw_win[:].bitcast(U32).indirect(entries(offs_sb, h * HALF, HALF))
@@ -120,17 +120,19 @@ def tile_picked_temper_tanh_p_kernel(
                 stop=True,
             )
 
-        s_sb = [sb.tile([P, PACK, HALF], F32, name=f"s_sb{h}", tag=f"s_sb{h}", align_bytes=64) for h in range(2)]
-        for b, (h, t0, slots) in enumerate(((0, 0, 1), (0, 1, 1), (0, 2, 2), (1, 0, 2), (1, 2, 2))):
-            bank = ps.tile([P, slots, HALF], F32, name=f"s_bank{b}", tag=f"bank{b}")
-            for e in range(slots):
-                score(bank[:, e, :], h, t0 + e)
-            nc.scalar.copy(s_sb[h][:, t0 : t0 + slots, :], bank[:])
+        banks = (((0, 0),), ((0, 1),), ((1, 0), (0, 2)), ((0, 3), (1, 1)), ((1, 2), (1, 3)))
+        s_sb = {}
+        for b, passes in enumerate(banks):
+            bank = ps.tile([P, len(passes), HALF], F32, name=f"s_bank{b}", tag=f"bank{b}")
+            scores = sb.tile([P, len(passes), HALF], F32, name=f"s_sb{b}", align_bytes=64)
+            for e, (h, t) in enumerate(passes):
+                score(bank[:, e, :], h, t)
+                s_sb[h, t] = scores[:, e, :]
+            nc.scalar.copy(scores[:], bank[:])
 
-        def temper(y, h):
-            for t in range(PACK):
-                looked_up = temp_win[t][:].indirect(entries(task_sb, h * HALF, HALF))
-                nc.vector.tensor_tensor(y[:, t, :], looked_up, s_sb[h][:, t, :], MULT)
+        def temper(y, h, t):
+            looked_up = temp_win[t][:].indirect(entries(task_sb, h * HALF, HALF))
+            nc.vector.tensor_tensor(y[:, t, :], looked_up, s_sb[h, t], MULT)
 
         def squash(th, y):
             nc.scalar.activation(
@@ -178,31 +180,32 @@ def tile_picked_temper_tanh_p_kernel(
         ths = [P, CH, PACK]
         vcopy, scopy = nc.vector.tensor_copy, nc.scalar.copy
         ya = shared.tile([P, PACK, HALF], F32, name="ya", align_bytes=64, offset=20480)
-        temper(ya, 0)
         yb = shared.tile([P, PACK, HALF], F32, name="yb", align_bytes=64, offset=28672)
-        temper(yb, 1)
+        for passes in banks:
+            for h, t in passes:
+                temper((ya, yb)[h], h, t)
         wa = ring("wa", [P, HALF, PACK], BF16, "wa")
         weave(wa[:], w_raw[0][:])
-        th01 = shared.tile([P, HALF, PACK], F32, name="th01", align_bytes=64, offset=6144 + 2048)
+        th01 = shared.tile([P, HALF, PACK], F32, name="th01", align_bytes=64, offset=16384)
         squash(th01[:], ya[:])
-        wb = shared.tile([P, HALF, PACK], BF16, name="wb", align_bytes=64, offset=6144)
+        wb = ring("xw_got", [P, HALF, PACK], BF16, "wb")
         weave(wb[:], w_raw[1][:])
         th2 = shared.tile(ths, F32, name="th2", align_bytes=64, offset=20480 + 1024)
         squash(th2[:], yb[:, :, 0:CH])
         th3 = shared.tile(ths, F32, name="th3", align_bytes=64, offset=24576 - 512)
         squash(th3[:], yb[:, :, CH:HALF])
-        qa = quantise(wa[:], "wa", 16384)
         z01 = ring("z01", [P, HALF, PACK], BF16, "z01")
         weigh(z01[:], th01[:])
-        qb = quantise(wb[:], "wb", 18432)
-        q01 = quantise(z01[:], "z01", 17408)
+        qa = quantise(wa[:], "wa", 20480)
+        q01 = quantise(z01[:], "z01", 26624)
+        qb = quantise(wb[:], "wb", 16384)
         qw = [(qa, 0), (qa, P), (qb, 0), (qb, P)]
         z2 = ring("z2", ths, BF16, "z2")
         weigh(z2[:], th2[:])
         z3 = ring("z3", ths, BF16, "z3")
         weigh(z3[:], th3[:])
         q2 = quantise(z2[:], "z2", 28672)
-        q3 = quantise(z3[:], "z3", 19968)
+        q3 = quantise(z3[:], "z3", 27648)
         for block, bank in enumerate(("bank5", "bank6", "bank7", "bank0")):
             project(ring(f"res_a{block}", [P, 1, HALF], F32, f"res_a{block}"), 0, q01, qw, block, bank, scopy)
         project(ring("res_2a", [P, 2, CH], F32, "res_2a"), 2 * CH, q2, qw, 0, "bank1", scopy)

@@ -171,8 +171,11 @@ def tile_picked_temper_tanh_p_kernel(
                     start=True,
                     stop=True,
                 )
-            copy(res[:], bank[:])
-            nc.sync.dma_start(out_rows[:, b0 : b0 + blocks, j0 : j0 + n], res[:])
+            copy(res, bank[:])
+
+        def store(res, j0, b0):
+            blocks, n = res.shape[1], res.shape[2]
+            nc.sync.dma_start(out_rows[:, b0 : b0 + blocks, j0 : j0 + n], res)
 
         def ring(tag, shape, dtype, name):
             return sb.tile(shape, dtype, name=name, tag=tag, align_bytes=64)
@@ -200,15 +203,26 @@ def tile_picked_temper_tanh_p_kernel(
         q01 = quantise(z01[:], "z01", 26624)
         qb = quantise(wb[:], "wb", 16384)
         qw = [(qa, 0), (qa, P), (qb, 0), (qb, P)]
-        z2 = ring("z2", ths, BF16, "z2")
+        z2 = shared.tile(ths, BF16, name="z2", align_bytes=64, offset=32768)
         weigh(z2[:], th2[:])
         z3 = ring("z3", ths, BF16, "z3")
         weigh(z3[:], th3[:])
         q2 = quantise(z2[:], "z2", 28672)
         q3 = quantise(z3[:], "z3", 27648)
-        for block, bank in enumerate(("bank5", "bank6", "bank7", "bank0")):
-            project(ring(f"res_a{block}", [P, 1, HALF], F32, f"res_a{block}"), 0, q01, qw, block, bank, scopy)
-        project(ring("res_2a", [P, 2, CH], F32, "res_2a"), 2 * CH, q2, qw, 0, "bank1", scopy)
-        project(ring("res_2b", [P, 2, CH], F32, "res_2b"), 2 * CH, q2, qw, 2, "bank2", vcopy)
-        project(ring("res_3a", [P, 2, CH], F32, "res_3a"), 3 * CH, q3, qw, 0, "bank3", scopy)
-        project(ring("res_3b", [P, 2, CH], F32, "res_3b"), 3 * CH, q3, qw, 2, "bank4", vcopy)
+        for b0, banks_a in ((0, ("bank5",)), (1, ("bank6", "bank7"))):
+            res = ring(f"res_a{b0}", [P, len(banks_a), HALF], F32, f"res_a{b0}")
+            for e in range(len(banks_a)):
+                project(res[:, e : e + 1, :], 0, q01, qw, b0 + e, banks_a[e], scopy)
+            store(res[:], 0, b0)
+        res = shared.tile([P, 1, HALF], F32, name="res_a3", align_bytes=64, offset=32768)
+        project(res[:], 0, q01, qw, 3, "bank0", vcopy)
+        store(res[:], 0, 3)
+        for b0, bank, copy in ((0, "bank1", scopy), (2, "bank2", vcopy)):
+            res = ring(f"res_b{b0}", [P, 2, CH], F32, f"res_b{b0}")
+            project(res[:], 2 * CH, q2, qw, b0, bank, copy)
+            store(res[:], 2 * CH, b0)
+        for b0, banks_c in ((0, ("bank3", "bank4")), (2, ("bank5", "bank6"))):
+            res = ring(f"res_c{b0}", [P, 2, CH], F32, f"res_c{b0}")
+            for e, copy in enumerate((scopy, vcopy)):
+                project(res[:, e : e + 1, :], 3 * CH, q3, qw, b0 + e, banks_c[e], copy)
+            store(res[:], 3 * CH, b0)

@@ -124,7 +124,7 @@ def tile_picked_temper_tanh_p_kernel(
         s_sb = {}
         for b, passes in enumerate(banks):
             bank = ps.tile([P, len(passes), HALF], F32, name=f"s_bank{b}", tag=f"bank{b}")
-            scores = sb.tile([P, len(passes), HALF], F32, name=f"s_sb{b}", align_bytes=64)
+            scores = sb.tile([P, len(passes), HALF], F32, name=f"s_sb{b}", tag=f"s_sb{b}", align_bytes=64)
             for e, (h, t) in enumerate(passes):
                 score(bank[:, e, :], h, t)
                 s_sb[h, t] = scores[:, e, :]
@@ -191,17 +191,28 @@ def tile_picked_temper_tanh_p_kernel(
         weave(wa[:], w_raw[0][:])
         th01 = shared.tile([P, HALF, PACK], F32, name="th01", align_bytes=64, offset=16384)
         squash(th01[:], ya[:])
-        wb = ring("xw_got", [P, HALF, PACK], BF16, "wb")
+        wb = ring("s_sb3", [P, HALF, PACK], BF16, "wb")
         weave(wb[:], w_raw[1][:])
         th2 = shared.tile(ths, F32, name="th2", align_bytes=64, offset=20480 + 1024)
         squash(th2[:], yb[:, :, 0:CH])
         th3 = shared.tile(ths, F32, name="th3", align_bytes=64, offset=24576 - 512)
         squash(th3[:], yb[:, :, CH:HALF])
+        qa = quantise(wa[:], "wa", 6144)
+        warm = ps.tile([P, S], F32, name="warm", tag="bank1")
+        for e in range(2):
+            nc.tensor.matmul_mx(
+                out=warm[:],
+                lhsT=qa[0][:, e * P : (e + 1) * P].bitcast(FP8X4),
+                lhsT_scale=qa[1][:, e * P : (e + 1) * P],
+                rhs=xw_got[:].bitcast(FP8X4),
+                rhs_scale=planes[:, H : H + S],
+                start=True,
+                stop=True,
+            )
         z01 = ring("z01", [P, HALF, PACK], BF16, "z01")
         weigh(z01[:], th01[:])
-        qa = quantise(wa[:], "wa", 20480)
+        qb = quantise(wb[:], "wb", 20480)
         q01 = quantise(z01[:], "z01", 26624)
-        qb = quantise(wb[:], "wb", 16384)
         qw = [(qa, 0), (qa, P), (qb, 0), (qb, P)]
         z2 = shared.tile(ths, BF16, name="z2", align_bytes=64, offset=32768)
         weigh(z2[:], th2[:])

@@ -45,7 +45,6 @@ def tile_picked_temper_tanh_p_kernel(
         nc.sync.dma_start(dsc_win[:].bitcast(I32), d_scales[0].bitcast(I32).unsqueeze(1).to_broadcast(spread))
         nc.sync.dma_start(offs_sb[:], offs)
         nc.sync.dma_start(xsc_win[0:P:8, :].bitcast(I32), x_scales[0].bitcast(I32))
-        nc.sync.dma_start(task_sb[:], task)
 
         dw_win = shared.tile([P, TABLE], I32, name="dw_win", align_bytes=64, offset=6144)
         xw_win = sb.tile([P, TABLE], I32, name="xw_win", align_bytes=64)
@@ -60,6 +59,7 @@ def tile_picked_temper_tanh_p_kernel(
             return win
 
         temp_win = [load_temp(0, 14336)]
+        nc.sync.dma_start(task_sb[:], task)
 
         dsc_got = sb.tile([P, H], U8, name="dsc_got", align_bytes=64)
         xsc_got = shared.tile([P, S], U8, name="xsc_got", align_bytes=64, offset=1792)
@@ -232,8 +232,10 @@ def tile_picked_temper_tanh_p_kernel(
             res = ring(f"res_b{b0}", [P, 2, CH], F32, f"res_b{b0}")
             project(res[:], 2 * CH, q2, qw, b0, bank, copy)
             store(res[:], 2 * CH, b0)
-        for b0, banks_c in ((0, ("bank3", "bank4")), (2, ("bank5", "bank6"))):
-            res = ring(f"res_c{b0}", [P, 2, CH], F32, f"res_c{b0}")
-            for e, copy in enumerate((scopy, vcopy)):
-                project(res[:, e : e + 1, :], 3 * CH, q3, qw, b0 + e, banks_c[e], copy)
-            store(res[:], 3 * CH, b0)
+        res = ring("res_c0", [P, 2, CH], F32, "res_c0")
+        for block, bank, copy in ((0, "bank3", scopy), (1, "bank4", vcopy)):
+            project(res[:, block : block + 1, :], 3 * CH, q3, qw, block, bank, copy)
+        store(res[:], 3 * CH, 0)
+        res = ring("res_c2", [P, 2, CH], F32, "res_c2")
+        project(res[:], 3 * CH, q3, qw, 2, "bank5", scopy)
+        store(res[:], 3 * CH, 2)

@@ -148,12 +148,21 @@ def tile_picked_temper_tanh_p_kernel(
         def weave(woven, src):
             nc.scalar.copy(woven.rearrange("p (c i) t -> p c t i", i=4), src.rearrange("p t (c i) -> p c t i", i=4))
 
-        def quantise(woven, label, offset):
-            n = woven.shape[1]
-            codes = shared.tile([P, n], U32, name=f"codes_{label}", align_bytes=64, offset=offset)
-            scales = sb.tile([P, n], U8, name=f"scales_{label}", align_bytes=64)
-            nc.vector.quantize_mx(out=codes[:].bitcast(FP8X4), scales=scales[:], in_=woven.rearrange("p n t -> p (n t)"))
+        def mx_tiles(label, offset):
+            codes = shared.tile([P, HALF], U32, name=f"codes_{label}", align_bytes=64, offset=offset)
+            scales = sb.tile([P, HALF], U8, name=f"scales_{label}", align_bytes=64)
             return codes, scales
+
+        def quantise_into(q, c0, woven):
+            cols = slice(c0, c0 + woven.shape[1])
+            nc.vector.quantize_mx(
+                out=q[0][:, cols].bitcast(FP8X4), scales=q[1][:, cols], in_=woven.rearrange("p n t -> p (n t)")
+            )
+
+        def quantise(woven, label, offset):
+            q = mx_tiles(label, offset)
+            quantise_into(q, 0, woven)
+            return q
 
         out_rows = out.rearrange("(b p) j -> p b j", p=P)
 
@@ -218,8 +227,9 @@ def tile_picked_temper_tanh_p_kernel(
         weigh(z2[:], th2[:])
         z3 = ring("z3", ths, BF16, "z3")
         weigh(z3[:], th3[:])
-        q2 = quantise(z2[:], "z2", 28672)
-        q3 = quantise(z3[:], "z3", 27648)
+        q23 = mx_tiles("z23", 28672)
+        quantise_into(q23, 0, z2[:])
+        quantise_into(q23, CH, z3[:])
         for b0, banks_a in ((0, ("bank5",)), (1, ("bank6", "bank7"))):
             res = ring(f"res_a{b0}", [P, len(banks_a), HALF], F32, f"res_a{b0}")
             for e in range(len(banks_a)):
@@ -228,14 +238,7 @@ def tile_picked_temper_tanh_p_kernel(
         res = shared.tile([P, 1, HALF], F32, name="res_a3", align_bytes=64, offset=32768)
         project(res[:], 0, q01, qw, 3, "bank0", vcopy)
         store(res[:], 0, 3)
-        for b0, bank, copy in ((0, "bank1", scopy), (2, "bank2", vcopy)):
-            res = ring(f"res_b{b0}", [P, 2, CH], F32, f"res_b{b0}")
-            project(res[:], 2 * CH, q2, qw, b0, bank, copy)
-            store(res[:], 2 * CH, b0)
-        res = ring("res_c0", [P, 2, CH], F32, "res_c0")
-        for block, bank, copy in ((0, "bank3", scopy), (1, "bank4", vcopy)):
-            project(res[:, block : block + 1, :], 3 * CH, q3, qw, block, bank, copy)
-        store(res[:], 3 * CH, 0)
-        res = ring("res_c2", [P, 2, CH], F32, "res_c2")
-        project(res[:], 3 * CH, q3, qw, 2, "bank5", scopy)
-        store(res[:], 3 * CH, 2)
+        for block, bank in enumerate(("bank1", "bank2", "bank3", "bank4")):
+            res = ring(f"res_b{block}", [P, 1, HALF], F32, f"res_b{block}")
+            project(res[:], HALF, q23, qw, block, bank, (scopy, vcopy)[block % 2])
+            store(res[:], HALF, block)

@@ -166,7 +166,7 @@ def tile_picked_temper_tanh_p_kernel(
 
         out_rows = out.rearrange("(b p) j -> p b j", p=P)
 
-        def project(res, j0, z_q, w_qs, b0, bank_tag, copy):
+        def project(res, j0, z_q, w_qs, b0, bank_tag, copy, c0=0):
             blocks, n = res.shape[1], res.shape[2]
             bank = ps.tile([P, blocks, n], F32, name=f"o_bank{j0}_{b0}", tag=bank_tag)
             for e in range(blocks):
@@ -175,8 +175,8 @@ def tile_picked_temper_tanh_p_kernel(
                     out=bank[:, e, :],
                     lhsT=w_q[0][:, m0 : m0 + P].bitcast(FP8X4),
                     lhsT_scale=w_q[1][:, m0 : m0 + P],
-                    rhs=z_q[0][:].bitcast(FP8X4),
-                    rhs_scale=z_q[1][:],
+                    rhs=z_q[0][:, c0 : c0 + n].bitcast(FP8X4),
+                    rhs_scale=z_q[1][:, c0 : c0 + n],
                     start=True,
                     stop=True,
                 )
@@ -238,7 +238,10 @@ def tile_picked_temper_tanh_p_kernel(
         res = shared.tile([P, 1, HALF], F32, name="res_a3", align_bytes=64, offset=32768)
         project(res[:], 0, q01, qw, 3, "bank0", vcopy)
         store(res[:], 0, 3)
-        for block, bank in enumerate(("bank1", "bank2", "bank3", "bank4")):
-            res = ring(f"res_b{block}", [P, 1, HALF], F32, f"res_b{block}")
-            project(res[:], HALF, q23, qw, block, bank, (scopy, vcopy)[block % 2])
-            store(res[:], HALF, block)
+        res_b = ring("res_b", [P, PACK, HALF], F32, "res_b")
+        for b0, bank, copy in ((0, "bank1", scopy), (2, "bank2", scopy)):
+            project(res_b[:, b0 : b0 + 2, 0:CH], HALF, q23, qw, b0, bank, copy)
+        for block, bank in enumerate(("bank3", "bank4", "bank5", "bank6")):
+            copy = scopy if block == PACK - 1 else vcopy
+            project(res_b[:, block : block + 1, CH:HALF], HALF + CH, q23, qw, block, bank, copy, CH)
+            store(res_b[:, block : block + 1, :], HALF, block)

@@ -41,8 +41,8 @@ def tile_picked_temper_tanh_p_kernel(
         xsc_win = sb.tile([P, TABLE], U8, name="xsc_win", align_bytes=64)
         spread = [16, 8, TABLE // 4]
         nc.vector.memset(xsc_win[:].bitcast(I32), 0)
-        nc.sync.dma_start(kidx_sb[:], kidx)
         nc.sync.dma_start(dsc_win[:].bitcast(I32), d_scales[0].bitcast(I32).unsqueeze(1).to_broadcast(spread))
+        nc.sync.dma_start(kidx_sb[:], kidx)
         nc.sync.dma_start(offs_sb[:], offs)
         nc.sync.dma_start(xsc_win[0:P:8, :].bitcast(I32), x_scales[0].bitcast(I32))
 

@@ -21,6 +21,7 @@ N = 512
 U = 512
 HALF = 256
 CH = 128
+SPLIT = 128
 FLOPS = 2 * 512 * H * S + 2 * H * N * S
 
 
@@ -39,18 +40,11 @@ def tile_picked_temper_tanh_p_kernel(
         task_sb = lists.tile([P, S // 16], U16, name="task_sb")
         dsc_win = sb.tile([P, TABLE], U8, name="dsc_win", align_bytes=64)
         xsc_win = sb.tile([P, TABLE], U8, name="xsc_win", align_bytes=64)
-        spread = [16, 8, TABLE // 4]
-        nc.vector.memset(xsc_win[:].bitcast(I32), 0)
-        nc.sync.dma_start(dsc_win[:].bitcast(I32), d_scales[0].bitcast(I32).unsqueeze(1).to_broadcast(spread))
-        nc.sync.dma_start(kidx_sb[:], kidx)
-        nc.sync.dma_start(offs_sb[:], offs)
-        nc.sync.dma_start(xsc_win[0:P:8, :].bitcast(I32), x_scales[0].bitcast(I32))
+        nc.vector.memset(dsc_win[:].bitcast(I32), 0)
+        nc.gpsimd.memset(xsc_win[:].bitcast(I32), 0)
 
-        dw_win = shared.tile([P, TABLE], I32, name="dw_win", align_bytes=64, offset=6144)
+        dw_win = shared.tile([P, TABLE], I32, name="dw_win", align_bytes=64, offset=57344)
         xw_win = sb.tile([P, TABLE], I32, name="xw_win", align_bytes=64)
-        nc.sync.dma_start(dw_win[:], d_words[0].rearrange("p n t -> p (n t)").bitcast(I32))
-        nc.sync.dma_start(xw_win[:], x_words[0].rearrange("p n t -> p (n t)").bitcast(I32))
-
         temp_rows = temp.rearrange("(p t) u -> p t u", t=PACK)
 
         def load_temp(t, offset):
@@ -58,8 +52,17 @@ def tile_picked_temper_tanh_p_kernel(
             nc.sync.dma_start(win[:], temp_rows[:, t, :])
             return win
 
-        temp_win = [load_temp(0, 14336)]
         nc.sync.dma_start(task_sb[:], task)
+        temp_win = [load_temp(0, 12288)]
+        nc.sync.dma_start(kidx_sb[:], kidx)
+        nc.sync.dma_start(offs_sb[:], offs)
+        nc.sync.dma_start(dsc_win[0:P:8, :].bitcast(I32), d_scales[0].bitcast(I32))
+        nc.sync.dma_start(xsc_win[0:P:8, :].bitcast(I32), x_scales[0].bitcast(I32))
+        temp_win.append(load_temp(1, 14336))
+        nc.sync.dma_start(dw_win[:], d_words[0].rearrange("p n t -> p (n t)").bitcast(I32))
+        temp_win.append(load_temp(2, 55296))
+        nc.sync.dma_start(xw_win[:], x_words[0].rearrange("p n t -> p (n t)").bitcast(I32))
+        temp_win.append(load_temp(3, 69632))
 
         dsc_got = sb.tile([P, H], U8, name="dsc_got", align_bytes=64)
         xsc_got = shared.tile([P, S], U8, name="xsc_got", align_bytes=64, offset=1792)
@@ -80,15 +83,8 @@ def tile_picked_temper_tanh_p_kernel(
         nc.vector.tensor_copy(planes[:, H : H + S].bitcast(I32), xsc_got[:].bitcast(I32))
         for r in range(1, PACK):
             nc.sync.dma_start(planes[r:P:32, :].bitcast(I32), planes[8 * r : P : 32, :].bitcast(I32))
-        temp_win.append(load_temp(1, 0))
-        w_rows = w1.rearrange("(p t) m -> p t m", t=PACK)
-        w_raw = [
-            shared.tile([P, PACK, HALF], F32, name="w_raw0", align_bytes=64, offset=2048),
-            sb.tile([P, PACK, HALF], F32, name="w_raw1", tag="dw_got", align_bytes=64),
-        ]
-        nc.sync.dma_start(w_raw[0][:], w_rows[:, :, 0:HALF])
 
-        dw_got = sb.tile([P, H], U32, name="dw_got", tag="dw_got", align_bytes=64)
+        dw_got = shared.tile([P, H], U32, name="dw_got", align_bytes=64, offset=65536)
         dw_dealt = shared.tile([P, H], U32, name="dw_dealt", align_bytes=64, offset=16384)
         for h in range(2):
             nc.vector.tensor_copy(
@@ -97,42 +93,62 @@ def tile_picked_temper_tanh_p_kernel(
             )
         for h in range(2):
             deal(dw_dealt[:], dw_got, h * HALF, HALF)
-        temp_win.append(load_temp(2, 6144))
-        temp_win.append(load_temp(3, 8192))
+        w_rows = w1.rearrange("(p t) m -> p t m", t=PACK)
+        w_raw = [
+            shared.tile([P, PACK, HALF], F32, name="w_raw0", align_bytes=64, offset=2048),
+            shared.tile([P, PACK, HALF], F32, name="w_raw1", align_bytes=64, offset=65536),
+        ]
+        nc.sync.dma_start(w_raw[0][:], w_rows[:, :, 0:HALF])
+        gn_sb = shared.tile([P, PACK], F32, name="gn_sb", align_bytes=64, offset=57344)
+        nc.sync.dma_start(gn_sb[:], gn[:, 0].rearrange("(p t) -> p t", t=PACK))
         nc.sync.dma_start(w_raw[1][:], w_rows[:, :, HALF:N])
 
-        xw_got = sb.tile([P, S], U32, name="xw_got", tag="xw_got", align_bytes=64)
+        xw_got = [
+            shared.tile([P, HALF], U32, name=f"xw_got{h}", align_bytes=64, offset=51200 + 2048 * h) for h in range(2)
+        ]
         for h in range(2):
-            nc.vector.tensor_copy(
-                xw_got[:, h * HALF : (h + 1) * HALF], xw_win[:].bitcast(U32).indirect(entries(offs_sb, h * HALF, HALF))
-            )
-        gn_sb = sb.tile([P, PACK], F32, name="gn_sb", tag="xw_win", align_bytes=64)
-        nc.sync.dma_start(gn_sb[:], gn[:, 0].rearrange("(p t) -> p t", t=PACK))
+            nc.vector.tensor_copy(xw_got[h][:], xw_win[:].bitcast(U32).indirect(entries(offs_sb, h * HALF, HALF)))
+
+        def look_up(got, h, t):
+            nc.scalar.activation(got, temp_win[t][:].indirect(entries(task_sb, h * HALF, HALF)), ACT.Copy)
 
         def score(dst, h, t):
             nc.tensor.matmul_mx(
                 out=dst,
                 lhsT=dw_dealt[:, t * P : (t + 1) * P].bitcast(FP8X4),
                 lhsT_scale=planes[:, t * P : (t + 1) * P],
-                rhs=xw_got[:, h * HALF : (h + 1) * HALF].bitcast(FP8X4),
+                rhs=xw_got[h][:].bitcast(FP8X4),
                 rhs_scale=planes[:, H + h * HALF : H + (h + 1) * HALF],
                 start=True,
                 stop=True,
             )
 
-        banks = (((0, 0),), ((0, 1),), ((1, 0), (0, 2)), ((0, 3), (1, 1)), ((1, 2), (1, 3)))
-        s_sb = {}
-        for b, passes in enumerate(banks):
-            bank = ps.tile([P, len(passes), HALF], F32, name=f"s_bank{b}", tag=f"bank{b}")
-            scores = sb.tile([P, len(passes), HALF], F32, name=f"s_sb{b}", tag=f"s_sb{b}", align_bytes=64)
-            for e, (h, t) in enumerate(passes):
-                score(bank[:, e, :], h, t)
-                s_sb[h, t] = scores[:, e, :]
-            nc.scalar.copy(scores[:], bank[:])
+        ya = shared.tile([P, PACK, HALF], F32, name="ya", align_bytes=64, offset=20480)
+        yb = shared.tile([P, PACK, HALF], F32, name="yb", align_bytes=64, offset=28672)
+        s_bank = {}
 
-        def temper(y, h, t):
-            looked_up = temp_win[t][:].indirect(entries(task_sb, h * HALF, HALF))
-            nc.vector.tensor_tensor(y[:, t, :], looked_up, s_sb[h, t], MULT)
+        def score_pair(h, t0, bank_tag):
+            s_bank[h, t0] = ps.tile([P, 2, HALF], F32, name=f"s_bank{h}{t0}", tag=bank_tag)
+            for e in range(2):
+                score(s_bank[h, t0][:, e, :], h, t0 + e)
+
+        score_pair(0, 0, "bank0")
+        score_pair(0, 2, "bank1")
+        score_pair(1, 2, "bank3")
+
+        def got_tile(label, slots, offset):
+            return shared.tile([P, slots, HALF], F32, name=f"got_{label}", align_bytes=64, offset=offset)
+
+        got_a01, got_b01, got_a23 = got_tile("a01", 2, 36864), got_tile("b01", 2, 38912), got_tile("a23", 2, 40960)
+        got_b23 = got_tile("b23", 2, 6144)
+        for t in range(PACK):
+            look_up((got_a01, got_a23)[t // 2][:, t % 2, :], 0, t)
+            look_up((got_b01, got_b23)[t // 2][:, t % 2, :], 1, t)
+        nc.vector.tensor_tensor(ya[:, 0:2, :], s_bank[0, 0][:], got_a01[:], MULT)
+        score_pair(1, 0, "bank0")
+        nc.vector.tensor_tensor(ya[:, 2:4, :], s_bank[0, 2][:], got_a23[:], MULT)
+        nc.vector.tensor_tensor(yb[:, 2:4, :], s_bank[1, 2][:], got_b23[:], MULT)
+        nc.vector.tensor_tensor(yb[:, 0:2, :], s_bank[1, 0][:], got_b01[:], MULT)
 
         def squash(th, y):
             nc.scalar.activation(
@@ -145,8 +161,8 @@ def tile_picked_temper_tanh_p_kernel(
         def weigh(z, th):
             nc.vector.tensor_tensor(z, th, gn_sb[:].unsqueeze(1).to_broadcast(list(th.shape)), MULT)
 
-        def weave(woven, src):
-            nc.scalar.copy(woven.rearrange("p (c i) t -> p c t i", i=4), src.rearrange("p t (c i) -> p c t i", i=4))
+        def weave(woven, src, copy):
+            copy(woven.rearrange("p (c i) t -> p c t i", i=4), src.rearrange("p t (c i) -> p c t i", i=4))
 
         def mx_tiles(label, offset):
             codes = shared.tile([P, HALF], U32, name=f"codes_{label}", align_bytes=64, offset=offset)
@@ -191,38 +207,25 @@ def tile_picked_temper_tanh_p_kernel(
 
         ths = [P, CH, PACK]
         vcopy, scopy = nc.vector.tensor_copy, nc.scalar.copy
-        ya = shared.tile([P, PACK, HALF], F32, name="ya", align_bytes=64, offset=20480)
-        yb = shared.tile([P, PACK, HALF], F32, name="yb", align_bytes=64, offset=28672)
-        for passes in banks:
-            for h, t in passes:
-                temper((ya, yb)[h], h, t)
-        wa = ring("wa", [P, HALF, PACK], BF16, "wa")
-        weave(wa[:], w_raw[0][:])
-        th01 = shared.tile([P, HALF, PACK], F32, name="th01", align_bytes=64, offset=16384)
+        wa = ring("wa", [P, SPLIT, PACK], BF16, "wa")
+        weave(wa[:], w_raw[0][:, :, 0:SPLIT], scopy)
+        th01 = shared.tile([P, HALF, PACK], F32, name="th01", align_bytes=64, offset=43008)
         squash(th01[:], ya[:])
-        wb = ring("s_sb3", [P, HALF, PACK], BF16, "wb")
-        weave(wb[:], w_raw[1][:])
-        th2 = shared.tile(ths, F32, name="th2", align_bytes=64, offset=20480 + 1024)
-        squash(th2[:], yb[:, :, 0:CH])
-        th3 = shared.tile(ths, F32, name="th3", align_bytes=64, offset=24576 - 512)
-        squash(th3[:], yb[:, :, CH:HALF])
-        qa = quantise(wa[:], "wa", 6144)
-        warm = ps.tile([P, S], F32, name="warm", tag="bank1")
-        for e in range(2):
-            nc.tensor.matmul_mx(
-                out=warm[:],
-                lhsT=qa[0][:, e * P : (e + 1) * P].bitcast(FP8X4),
-                lhsT_scale=qa[1][:, e * P : (e + 1) * P],
-                rhs=xw_got[:].bitcast(FP8X4),
-                rhs_scale=planes[:, H : H + S],
-                start=True,
-                stop=True,
-            )
+        wb = shared.tile([P, HALF, PACK], BF16, name="wb", align_bytes=64, offset=40960)
+        weave(wb[:], w_raw[1][:], scopy)
+        wa_end = shared.tile([P, HALF - SPLIT, PACK], BF16, name="wa_end", align_bytes=64, offset=6144)
+        weave(wa_end[:], w_raw[0][:, :, SPLIT:HALF], vcopy)
+        q0 = quantise(wa[:], "w0", 38912)
         z01 = ring("z01", [P, HALF, PACK], BF16, "z01")
         weigh(z01[:], th01[:])
-        qb = quantise(wb[:], "wb", 20480)
-        q01 = quantise(z01[:], "z01", 26624)
-        qw = [(qa, 0), (qa, P), (qb, 0), (qb, P)]
+        q1 = quantise(wa_end[:], "w1", 20480)
+        q01 = quantise(z01[:], "z01", 12288)
+        qb = quantise(wb[:], "wb", 43008)
+        th2 = shared.tile(ths, F32, name="th2", align_bytes=64, offset=47104)
+        squash(th2[:], yb[:, :, 0:CH])
+        th3 = shared.tile(ths, F32, name="th3", align_bytes=64, offset=49152)
+        squash(th3[:], yb[:, :, CH:HALF])
+        qw = [(q0, 0), (q1, 0), (qb, 0), (qb, P)]
         z2 = shared.tile(ths, BF16, name="z2", align_bytes=64, offset=32768)
         weigh(z2[:], th2[:])
         z3 = ring("z3", ths, BF16, "z3")

@@ -11,6 +11,7 @@ U8 = mybir.dt.uint8
 FP8X4 = mybir.dt.float8_e4m3fn_x4
 ACT = mybir.ActivationFunctionType
 MULT = mybir.AluOpType.mult
+ADD = mybir.AluOpType.add
 
 P = 128
 PACK = 4
@@ -52,17 +53,16 @@ def tile_picked_temper_tanh_p_kernel(
             nc.sync.dma_start(win[:], temp_rows[:, t, :])
             return win
 
-        nc.sync.dma_start(task_sb[:], task)
         temp_win = [load_temp(0, 12288)]
         nc.sync.dma_start(kidx_sb[:], kidx)
         nc.sync.dma_start(offs_sb[:], offs)
         nc.sync.dma_start(dsc_win[0:P:8, :].bitcast(I32), d_scales[0].bitcast(I32))
         nc.sync.dma_start(xsc_win[0:P:8, :].bitcast(I32), x_scales[0].bitcast(I32))
-        temp_win.append(load_temp(1, 14336))
+        nc.sync.dma_start(task_sb[:], task)
         nc.sync.dma_start(dw_win[:], d_words[0].rearrange("p n t -> p (n t)").bitcast(I32))
-        temp_win.append(load_temp(2, 55296))
+        temp_win.append(load_temp(1, 14336))
         nc.sync.dma_start(xw_win[:], x_words[0].rearrange("p n t -> p (n t)").bitcast(I32))
-        temp_win.append(load_temp(3, 69632))
+        temp_win.append(load_temp(2, 55296))
 
         dsc_got = sb.tile([P, H], U8, name="dsc_got", align_bytes=64)
         xsc_got = shared.tile([P, S], U8, name="xsc_got", align_bytes=64, offset=1792)
@@ -83,6 +83,7 @@ def tile_picked_temper_tanh_p_kernel(
         nc.vector.tensor_copy(planes[:, H : H + S].bitcast(I32), xsc_got[:].bitcast(I32))
         for r in range(1, PACK):
             nc.sync.dma_start(planes[r:P:32, :].bitcast(I32), planes[8 * r : P : 32, :].bitcast(I32))
+        temp_win.append(load_temp(3, 0))
 
         dw_got = shared.tile([P, H], U32, name="dw_got", align_bytes=64, offset=65536)
         dw_dealt = shared.tile([P, H], U32, name="dw_dealt", align_bytes=64, offset=16384)
@@ -127,14 +128,15 @@ def tile_picked_temper_tanh_p_kernel(
         yb = shared.tile([P, PACK, HALF], F32, name="yb", align_bytes=64, offset=28672)
         s_bank = {}
 
-        def score_pair(h, t0, bank_tag):
-            s_bank[h, t0] = ps.tile([P, 2, HALF], F32, name=f"s_bank{h}{t0}", tag=bank_tag)
-            for e in range(2):
+        def score_slots(h, t0, slots, bank_tag):
+            s_bank[h, t0] = ps.tile([P, slots, HALF], F32, name=f"s_bank{h}{t0}", tag=bank_tag)
+            for e in range(slots):
                 score(s_bank[h, t0][:, e, :], h, t0 + e)
 
-        score_pair(0, 0, "bank0")
-        score_pair(0, 2, "bank1")
-        score_pair(1, 2, "bank3")
+        score_slots(0, 0, 2, "bank0")
+        score_slots(0, 2, 1, "bank1")
+        score_slots(0, 3, 1, "bank2")
+        score_slots(1, 2, 2, "bank3")
 
         def got_tile(label, slots, offset):
             return shared.tile([P, slots, HALF], F32, name=f"got_{label}", align_bytes=64, offset=offset)
@@ -145,8 +147,9 @@ def tile_picked_temper_tanh_p_kernel(
             look_up((got_a01, got_a23)[t // 2][:, t % 2, :], 0, t)
             look_up((got_b01, got_b23)[t // 2][:, t % 2, :], 1, t)
         nc.vector.tensor_tensor(ya[:, 0:2, :], s_bank[0, 0][:], got_a01[:], MULT)
-        score_pair(1, 0, "bank0")
-        nc.vector.tensor_tensor(ya[:, 2:4, :], s_bank[0, 2][:], got_a23[:], MULT)
+        nc.vector.tensor_tensor(ya[:, 2:3, :], s_bank[0, 2][:], got_a23[:, 0:1, :], MULT)
+        score_slots(1, 0, 2, "bank1")
+        nc.vector.tensor_tensor(ya[:, 3:4, :], s_bank[0, 3][:], got_a23[:, 1:2, :], MULT)
         nc.vector.tensor_tensor(yb[:, 2:4, :], s_bank[1, 2][:], got_b23[:], MULT)
         nc.vector.tensor_tensor(yb[:, 0:2, :], s_bank[1, 0][:], got_b01[:], MULT)
 
@@ -207,44 +210,51 @@ def tile_picked_temper_tanh_p_kernel(
 
         ths = [P, CH, PACK]
         vcopy, scopy = nc.vector.tensor_copy, nc.scalar.copy
-        wa = ring("wa", [P, SPLIT, PACK], BF16, "wa")
-        weave(wa[:], w_raw[0][:, :, 0:SPLIT], scopy)
-        th01 = shared.tile([P, HALF, PACK], F32, name="th01", align_bytes=64, offset=43008)
-        squash(th01[:], ya[:])
-        wb = shared.tile([P, HALF, PACK], BF16, name="wb", align_bytes=64, offset=40960)
-        weave(wb[:], w_raw[1][:], scopy)
-        wa_end = shared.tile([P, HALF - SPLIT, PACK], BF16, name="wa_end", align_bytes=64, offset=6144)
-        weave(wa_end[:], w_raw[0][:, :, SPLIT:HALF], vcopy)
-        q0 = quantise(wa[:], "w0", 38912)
-        z01 = ring("z01", [P, HALF, PACK], BF16, "z01")
-        weigh(z01[:], th01[:])
-        q1 = quantise(wa_end[:], "w1", 20480)
-        q01 = quantise(z01[:], "z01", 12288)
-        qb = quantise(wb[:], "wb", 43008)
+        th0 = shared.tile(ths, F32, name="th0", align_bytes=64, offset=43008)
+        squash(th0[:], ya[:, :, 0:CH])
+        th1 = shared.tile(ths, F32, name="th1", align_bytes=64, offset=45056)
+        squash(th1[:], ya[:, :, CH:HALF])
+        wa = ring("wa", [P, HALF, PACK], BF16, "wa")
+        wb = ring("wb", [P, HALF, PACK], BF16, "wb")
+        for woven, raw, c0, c1 in ((wa, w_raw[0], 0, CH), (wa, w_raw[0], CH, HALF), (wb, w_raw[1], 0, SPLIT)):
+            nc.gpsimd.tensor_scalar(
+                woven[:, c0:c1, :], raw[:, :, c0:c1].rearrange("p t m -> p m t"), 1.0, 0.0, MULT, ADD
+            )
+        weave(wb[:, SPLIT:HALF, :], w_raw[1][:, :, SPLIT:HALF], scopy)
         th2 = shared.tile(ths, F32, name="th2", align_bytes=64, offset=47104)
         squash(th2[:], yb[:, :, 0:CH])
         th3 = shared.tile(ths, F32, name="th3", align_bytes=64, offset=49152)
         squash(th3[:], yb[:, :, CH:HALF])
-        qw = [(q0, 0), (q1, 0), (qb, 0), (qb, P)]
-        z2 = shared.tile(ths, BF16, name="z2", align_bytes=64, offset=32768)
+        z01 = ring("z01", [P, HALF, PACK], BF16, "z01")
+        weigh(z01[:, 0:CH, :], th0[:])
+        weigh(z01[:, CH:HALF, :], th1[:])
+        qa = quantise(wa[:], "wa", 20480)
+        q01 = quantise(z01[:], "z01", 12288)
+        z2 = shared.tile(ths, BF16, name="z2", align_bytes=64, offset=45056)
         weigh(z2[:], th2[:])
-        z3 = ring("z3", ths, BF16, "z3")
-        weigh(z3[:], th3[:])
-        q23 = mx_tiles("z23", 28672)
+        qb = quantise(wb[:], "wb", 46080)
+        qw = [(qa, 0), (qa, P), (qb, 0), (qb, P)]
+        q23 = mx_tiles("z23", 36864)
         quantise_into(q23, 0, z2[:])
+        z3 = shared.tile(ths, BF16, name="z3", align_bytes=64, offset=47104)
+        weigh(z3[:], th3[:])
+        for block, bank in ((0, "bank5"), (1, "bank6")):
+            res = ring(f"res_a{block}", [P, 1, HALF], F32, f"res_a{block}")
+            project(res[:], 0, q01, qw, block, bank, scopy)
+            store(res[:], 0, block)
+        res = shared.tile([P, 1, HALF], F32, name="res_a2", align_bytes=64, offset=45056)
+        project(res[:], 0, q01, qw, 2, "bank7", vcopy)
+        store(res[:], 0, 2)
         quantise_into(q23, CH, z3[:])
-        for b0, banks_a in ((0, ("bank5",)), (1, ("bank6", "bank7"))):
-            res = ring(f"res_a{b0}", [P, len(banks_a), HALF], F32, f"res_a{b0}")
-            for e in range(len(banks_a)):
-                project(res[:, e : e + 1, :], 0, q01, qw, b0 + e, banks_a[e], scopy)
-            store(res[:], 0, b0)
-        res = shared.tile([P, 1, HALF], F32, name="res_a3", align_bytes=64, offset=32768)
-        project(res[:], 0, q01, qw, 3, "bank0", vcopy)
+        res = ring("res_a3", [P, 1, HALF], F32, "res_a3")
+        project(res[:], 0, q01, qw, 3, "bank0", scopy)
         store(res[:], 0, 3)
-        res_b = ring("res_b", [P, PACK, HALF], F32, "res_b")
-        for b0, bank, copy in ((0, "bank1", scopy), (2, "bank2", scopy)):
-            project(res_b[:, b0 : b0 + 2, 0:CH], HALF, q23, qw, b0, bank, copy)
+        res_b = ring("res_b", [P, PACK, CH], F32, "res_b")
+        for b0, bank, copy in ((0, "bank1", scopy), (2, "bank2", vcopy)):
+            project(res_b[:, b0 : b0 + 2, :], HALF, q23, qw, b0, bank, copy)
+        store(res_b[:], HALF, 0)
+        res_c = ring("res_c", [P, PACK, CH], F32, "res_c")
         for block, bank in enumerate(("bank3", "bank4", "bank5", "bank6")):
-            copy = scopy if block == PACK - 1 else vcopy
-            project(res_b[:, block : block + 1, CH:HALF], HALF + CH, q23, qw, block, bank, copy, CH)
-            store(res_b[:, block : block + 1, :], HALF, block)
+            project(res_c[:, block : block + 1, :], HALF + CH, q23, qw, block, bank, (scopy, vcopy)[block % 2], CH)
+            if block % 2:
+                store(res_c[:, block - 1 : block + 1, :], HALF + CH, block - 1)

@@ -22,7 +22,6 @@ N = 512
 U = 512
 HALF = 256
 CH = 128
-SPLIT = 128
 FLOPS = 2 * 512 * H * S + 2 * H * N * S
 
 
@@ -61,8 +60,8 @@ def tile_picked_temper_tanh_p_kernel(
         nc.sync.dma_start(task_sb[:], task)
         nc.sync.dma_start(dw_win[:], d_words[0].rearrange("p n t -> p (n t)").bitcast(I32))
         temp_win.append(load_temp(1, 14336))
-        nc.sync.dma_start(xw_win[:], x_words[0].rearrange("p n t -> p (n t)").bitcast(I32))
         temp_win.append(load_temp(2, 55296))
+        nc.sync.dma_start(xw_win[:], x_words[0].rearrange("p n t -> p (n t)").bitcast(I32))
 
         dsc_got = sb.tile([P, H], U8, name="dsc_got", align_bytes=64)
         xsc_got = shared.tile([P, S], U8, name="xsc_got", align_bytes=64, offset=1792)
@@ -134,8 +133,7 @@ def tile_picked_temper_tanh_p_kernel(
                 score(s_bank[h, t0][:, e, :], h, t0 + e)
 
         score_slots(0, 0, 2, "bank0")
-        score_slots(0, 2, 1, "bank1")
-        score_slots(0, 3, 1, "bank2")
+        score_slots(0, 2, 2, "bank1")
         score_slots(1, 2, 2, "bank3")
 
         def got_tile(label, slots, offset):
@@ -146,12 +144,11 @@ def tile_picked_temper_tanh_p_kernel(
         for t in range(PACK):
             look_up((got_a01, got_a23)[t // 2][:, t % 2, :], 0, t)
             look_up((got_b01, got_b23)[t // 2][:, t % 2, :], 1, t)
-        nc.vector.tensor_tensor(ya[:, 0:2, :], s_bank[0, 0][:], got_a01[:], MULT)
-        nc.vector.tensor_tensor(ya[:, 2:3, :], s_bank[0, 2][:], got_a23[:, 0:1, :], MULT)
-        score_slots(1, 0, 2, "bank1")
-        nc.vector.tensor_tensor(ya[:, 3:4, :], s_bank[0, 3][:], got_a23[:, 1:2, :], MULT)
-        nc.vector.tensor_tensor(yb[:, 2:4, :], s_bank[1, 2][:], got_b23[:], MULT)
-        nc.vector.tensor_tensor(yb[:, 0:2, :], s_bank[1, 0][:], got_b01[:], MULT)
+        nc.vector.tensor_tensor(ya[:, 0:2, :], got_a01[:], s_bank[0, 0][:], MULT)
+        score_slots(1, 0, 2, "bank0")
+        nc.vector.tensor_tensor(ya[:, 2:4, :], got_a23[:], s_bank[0, 2][:], MULT)
+        nc.vector.tensor_tensor(yb[:, 2:4, :], got_b23[:], s_bank[1, 2][:], MULT)
+        nc.vector.tensor_tensor(yb[:, 0:2, :], got_b01[:], s_bank[1, 0][:], MULT)
 
         def squash(th, y):
             nc.scalar.activation(
@@ -215,21 +212,21 @@ def tile_picked_temper_tanh_p_kernel(
         th1 = shared.tile(ths, F32, name="th1", align_bytes=64, offset=45056)
         squash(th1[:], ya[:, :, CH:HALF])
         wa = ring("wa", [P, HALF, PACK], BF16, "wa")
-        wb = ring("wb", [P, HALF, PACK], BF16, "wb")
-        for woven, raw, c0, c1 in ((wa, w_raw[0], 0, CH), (wa, w_raw[0], CH, HALF), (wb, w_raw[1], 0, SPLIT)):
+        for c0 in (0, CH):
             nc.gpsimd.tensor_scalar(
-                woven[:, c0:c1, :], raw[:, :, c0:c1].rearrange("p t m -> p m t"), 1.0, 0.0, MULT, ADD
+                wa[:, c0 : c0 + CH, :], w_raw[0][:, :, c0 : c0 + CH].rearrange("p t m -> p m t"), 1.0, 0.0, MULT, ADD
             )
-        weave(wb[:, SPLIT:HALF, :], w_raw[1][:, :, SPLIT:HALF], scopy)
         th2 = shared.tile(ths, F32, name="th2", align_bytes=64, offset=47104)
         squash(th2[:], yb[:, :, 0:CH])
-        th3 = shared.tile(ths, F32, name="th3", align_bytes=64, offset=49152)
-        squash(th3[:], yb[:, :, CH:HALF])
-        z01 = ring("z01", [P, HALF, PACK], BF16, "z01")
+        wb = shared.tile([P, HALF, PACK], BF16, name="wb", align_bytes=64, offset=21504)
+        weave(wb[:], w_raw[1][:], scopy)
+        z01 = shared.tile([P, HALF, PACK], BF16, name="z01", align_bytes=64, offset=49152)
         weigh(z01[:, 0:CH, :], th0[:])
         weigh(z01[:, CH:HALF, :], th1[:])
         qa = quantise(wa[:], "wa", 20480)
         q01 = quantise(z01[:], "z01", 12288)
+        th3 = shared.tile(ths, F32, name="th3", align_bytes=64, offset=49152)
+        squash(th3[:], yb[:, :, CH:HALF])
         z2 = shared.tile(ths, BF16, name="z2", align_bytes=64, offset=45056)
         weigh(z2[:], th2[:])
         qb = quantise(wb[:], "wb", 46080)
@@ -238,10 +235,10 @@ def tile_picked_temper_tanh_p_kernel(
         quantise_into(q23, 0, z2[:])
         z3 = shared.tile(ths, BF16, name="z3", align_bytes=64, offset=47104)
         weigh(z3[:], th3[:])
+        res = ring("res_a0", [P, 2, HALF], F32, "res_a0")
         for block, bank in ((0, "bank5"), (1, "bank6")):
-            res = ring(f"res_a{block}", [P, 1, HALF], F32, f"res_a{block}")
-            project(res[:], 0, q01, qw, block, bank, scopy)
-            store(res[:], 0, block)
+            project(res[:, block : block + 1, :], 0, q01, qw, block, bank, scopy)
+        store(res[:], 0, 0)
         res = shared.tile([P, 1, HALF], F32, name="res_a2", align_bytes=64, offset=45056)
         project(res[:], 0, q01, qw, 2, "bank7", vcopy)
         store(res[:], 0, 2)
@@ -249,12 +246,9 @@ def tile_picked_temper_tanh_p_kernel(
         res = ring("res_a3", [P, 1, HALF], F32, "res_a3")
         project(res[:], 0, q01, qw, 3, "bank0", scopy)
         store(res[:], 0, 3)
-        res_b = ring("res_b", [P, PACK, CH], F32, "res_b")
-        for b0, bank, copy in ((0, "bank1", scopy), (2, "bank2", vcopy)):
-            project(res_b[:, b0 : b0 + 2, :], HALF, q23, qw, b0, bank, copy)
-        store(res_b[:], HALF, 0)
-        res_c = ring("res_c", [P, PACK, CH], F32, "res_c")
+        res_b = ring("res_b", [P, PACK, HALF], F32, "res_b")
+        for b0, bank, copy in ((0, "bank1", vcopy), (2, "bank2", scopy)):
+            project(res_b[:, b0 : b0 + 2, 0:CH], HALF, q23, qw, b0, bank, copy)
         for block, bank in enumerate(("bank3", "bank4", "bank5", "bank6")):
-            project(res_c[:, block : block + 1, :], HALF + CH, q23, qw, block, bank, (scopy, vcopy)[block % 2], CH)
-            if block % 2:
-                store(res_c[:, block - 1 : block + 1, :], HALF + CH, block - 1)
+            project(res_b[:, block : block + 1, CH:HALF], HALF + CH, q23, qw, block, bank, (vcopy, scopy)[block % 2], CH)
+            store(res_b[:, block : block + 1, :], HALF, block)

@@ -11,7 +11,6 @@ U8 = mybir.dt.uint8
 FP8X4 = mybir.dt.float8_e4m3fn_x4
 ACT = mybir.ActivationFunctionType
 MULT = mybir.AluOpType.mult
-ADD = mybir.AluOpType.add
 
 P = 128
 PACK = 4
@@ -52,16 +51,17 @@ def tile_picked_temper_tanh_p_kernel(
             nc.sync.dma_start(win[:], temp_rows[:, t, :])
             return win
 
+        nc.sync.dma_start(task_sb[:], task)
         temp_win = [load_temp(0, 12288)]
         nc.sync.dma_start(kidx_sb[:], kidx)
         nc.sync.dma_start(offs_sb[:], offs)
         nc.sync.dma_start(dsc_win[0:P:8, :].bitcast(I32), d_scales[0].bitcast(I32))
         nc.sync.dma_start(xsc_win[0:P:8, :].bitcast(I32), x_scales[0].bitcast(I32))
-        nc.sync.dma_start(task_sb[:], task)
-        nc.sync.dma_start(dw_win[:], d_words[0].rearrange("p n t -> p (n t)").bitcast(I32))
         temp_win.append(load_temp(1, 14336))
+        nc.sync.dma_start(dw_win[:], d_words[0].rearrange("p n t -> p (n t)").bitcast(I32))
         temp_win.append(load_temp(2, 55296))
         nc.sync.dma_start(xw_win[:], x_words[0].rearrange("p n t -> p (n t)").bitcast(I32))
+        temp_win.append(load_temp(3, 69632))
 
         dsc_got = sb.tile([P, H], U8, name="dsc_got", align_bytes=64)
         xsc_got = shared.tile([P, S], U8, name="xsc_got", align_bytes=64, offset=1792)
@@ -82,7 +82,6 @@ def tile_picked_temper_tanh_p_kernel(
         nc.vector.tensor_copy(planes[:, H : H + S].bitcast(I32), xsc_got[:].bitcast(I32))
         for r in range(1, PACK):
             nc.sync.dma_start(planes[r:P:32, :].bitcast(I32), planes[8 * r : P : 32, :].bitcast(I32))
-        temp_win.append(load_temp(3, 0))
 
         dw_got = shared.tile([P, H], U32, name="dw_got", align_bytes=64, offset=65536)
         dw_dealt = shared.tile([P, H], U32, name="dw_dealt", align_bytes=64, offset=16384)
@@ -207,15 +206,14 @@ def tile_picked_temper_tanh_p_kernel(
 
         ths = [P, CH, PACK]
         vcopy, scopy = nc.vector.tensor_copy, nc.scalar.copy
+        w0 = ring("w0", ths, BF16, "w0")
+        weave(w0[:], w_raw[0][:, :, 0:CH], scopy)
         th0 = shared.tile(ths, F32, name="th0", align_bytes=64, offset=43008)
         squash(th0[:], ya[:, :, 0:CH])
         th1 = shared.tile(ths, F32, name="th1", align_bytes=64, offset=45056)
         squash(th1[:], ya[:, :, CH:HALF])
-        wa = ring("wa", [P, HALF, PACK], BF16, "wa")
-        for c0 in (0, CH):
-            nc.gpsimd.tensor_scalar(
-                wa[:, c0 : c0 + CH, :], w_raw[0][:, :, c0 : c0 + CH].rearrange("p t m -> p m t"), 1.0, 0.0, MULT, ADD
-            )
+        w1_woven = shared.tile(ths, BF16, name="w1_woven", align_bytes=64, offset=6144)
+        weave(w1_woven[:], w_raw[0][:, :, CH:HALF], vcopy)
         th2 = shared.tile(ths, F32, name="th2", align_bytes=64, offset=47104)
         squash(th2[:], yb[:, :, 0:CH])
         wb = shared.tile([P, HALF, PACK], BF16, name="wb", align_bytes=64, offset=21504)
@@ -223,7 +221,9 @@ def tile_picked_temper_tanh_p_kernel(
         z01 = shared.tile([P, HALF, PACK], BF16, name="z01", align_bytes=64, offset=49152)
         weigh(z01[:, 0:CH, :], th0[:])
         weigh(z01[:, CH:HALF, :], th1[:])
-        qa = quantise(wa[:], "wa", 20480)
+        qa = mx_tiles("wa", 20480)
+        quantise_into(qa, 0, w0[:])
+        quantise_into(qa, CH, w1_woven[:])
         q01 = quantise(z01[:], "z01", 12288)
         th3 = shared.tile(ths, F32, name="th3", align_bytes=64, offset=49152)
         squash(th3[:], yb[:, :, CH:HALF])

@@ -57,14 +57,14 @@ def tile_picked_temper_tanh_p_kernel(
         nc.sync.dma_start(offs_sb[:], offs)
         nc.sync.dma_start(dsc_win[0:P:8, :].bitcast(I32), d_scales[0].bitcast(I32))
         nc.sync.dma_start(xsc_win[0:P:8, :].bitcast(I32), x_scales[0].bitcast(I32))
-        temp_win.append(load_temp(1, 14336))
         nc.sync.dma_start(dw_win[:], d_words[0].rearrange("p n t -> p (n t)").bitcast(I32))
+        temp_win.append(load_temp(1, 14336))
         temp_win.append(load_temp(2, 55296))
         nc.sync.dma_start(xw_win[:], x_words[0].rearrange("p n t -> p (n t)").bitcast(I32))
         temp_win.append(load_temp(3, 69632))
 
         dsc_got = sb.tile([P, H], U8, name="dsc_got", align_bytes=64)
-        xsc_got = shared.tile([P, S], U8, name="xsc_got", align_bytes=64, offset=1792)
+        xsc_got = sb.tile([P, S], U8, name="xsc_got", align_bytes=64)
 
         def entries(lst, j0, n):
             return lst[:, j0 // 16 : (j0 + n) // 16]
@@ -81,7 +81,7 @@ def tile_picked_temper_tanh_p_kernel(
         deal(planes[:, 0:H], dsc_got, 0, H)
         nc.vector.tensor_copy(planes[:, H : H + S].bitcast(I32), xsc_got[:].bitcast(I32))
         for r in range(1, PACK):
-            nc.sync.dma_start(planes[r:P:32, :].bitcast(I32), planes[8 * r : P : 32, :].bitcast(I32))
+            nc.scalar.dma_start(planes[r:P:32, :].bitcast(I32), planes[8 * r : P : 32, :].bitcast(I32))
 
         dw_got = shared.tile([P, H], U32, name="dw_got", align_bytes=64, offset=65536)
         dw_dealt = shared.tile([P, H], U32, name="dw_dealt", align_bytes=64, offset=16384)
@@ -94,7 +94,7 @@ def tile_picked_temper_tanh_p_kernel(
             deal(dw_dealt[:], dw_got, h * HALF, HALF)
         w_rows = w1.rearrange("(p t) m -> p t m", t=PACK)
         w_raw = [
-            shared.tile([P, PACK, HALF], F32, name="w_raw0", align_bytes=64, offset=2048),
+            shared.tile([P, PACK, HALF], F32, name="w_raw0", align_bytes=64, offset=61440),
             shared.tile([P, PACK, HALF], F32, name="w_raw1", align_bytes=64, offset=65536),
         ]
         nc.sync.dma_start(w_raw[0][:], w_rows[:, :, 0:HALF])
@@ -105,19 +105,22 @@ def tile_picked_temper_tanh_p_kernel(
         xw_got = [
             shared.tile([P, HALF], U32, name=f"xw_got{h}", align_bytes=64, offset=51200 + 2048 * h) for h in range(2)
         ]
-        for h in range(2):
-            nc.vector.tensor_copy(xw_got[h][:], xw_win[:].bitcast(U32).indirect(entries(offs_sb, h * HALF, HALF)))
+        for j0, n in ((0, CH), (CH, CH), (HALF, HALF)):
+            nc.vector.tensor_copy(
+                xw_got[j0 // HALF][:, j0 % HALF : j0 % HALF + n], xw_win[:].bitcast(U32).indirect(entries(offs_sb, j0, n))
+            )
 
-        def look_up(got, h, t):
-            nc.scalar.activation(got, temp_win[t][:].indirect(entries(task_sb, h * HALF, HALF)), ACT.Copy)
+        def look_up(got, t, j0):
+            nc.scalar.activation(got, temp_win[t][:].indirect(entries(task_sb, j0, got.shape[1])), ACT.Copy)
 
-        def score(dst, h, t):
+        def score(dst, t, j0):
+            n = dst.shape[1]
             nc.tensor.matmul_mx(
                 out=dst,
                 lhsT=dw_dealt[:, t * P : (t + 1) * P].bitcast(FP8X4),
                 lhsT_scale=planes[:, t * P : (t + 1) * P],
-                rhs=xw_got[h][:].bitcast(FP8X4),
-                rhs_scale=planes[:, H + h * HALF : H + (h + 1) * HALF],
+                rhs=xw_got[j0 // HALF][:, j0 % HALF : j0 % HALF + n].bitcast(FP8X4),
+                rhs_scale=planes[:, H + j0 : H + j0 + n],
                 start=True,
                 stop=True,
             )
@@ -126,28 +129,30 @@ def tile_picked_temper_tanh_p_kernel(
         yb = shared.tile([P, PACK, HALF], F32, name="yb", align_bytes=64, offset=28672)
         s_bank = {}
 
-        def score_slots(h, t0, slots, bank_tag):
-            s_bank[h, t0] = ps.tile([P, slots, HALF], F32, name=f"s_bank{h}{t0}", tag=bank_tag)
+        def score_slots(j0, n, t0, slots, bank_tag):
+            s_bank[j0, t0] = ps.tile([P, slots, n], F32, name=f"s_bank{j0}_{t0}", tag=bank_tag)
             for e in range(slots):
-                score(s_bank[h, t0][:, e, :], h, t0 + e)
+                score(s_bank[j0, t0][:, e, :], t0 + e, j0)
 
-        score_slots(0, 0, 2, "bank0")
-        score_slots(0, 2, 2, "bank1")
-        score_slots(1, 2, 2, "bank3")
+        score_slots(0, CH, 0, PACK, "bank0")
+        score_slots(CH, CH, 0, PACK, "bank1")
+        score_slots(HALF, HALF, 2, 2, "bank3")
 
         def got_tile(label, slots, offset):
             return shared.tile([P, slots, HALF], F32, name=f"got_{label}", align_bytes=64, offset=offset)
 
-        got_a01, got_b01, got_a23 = got_tile("a01", 2, 36864), got_tile("b01", 2, 38912), got_tile("a23", 2, 40960)
-        got_b23 = got_tile("b23", 2, 6144)
-        for t in range(PACK):
-            look_up((got_a01, got_a23)[t // 2][:, t % 2, :], 0, t)
-            look_up((got_b01, got_b23)[t // 2][:, t % 2, :], 1, t)
-        nc.vector.tensor_tensor(ya[:, 0:2, :], got_a01[:], s_bank[0, 0][:], MULT)
-        score_slots(1, 0, 2, "bank0")
-        nc.vector.tensor_tensor(ya[:, 2:4, :], got_a23[:], s_bank[0, 2][:], MULT)
-        nc.vector.tensor_tensor(yb[:, 2:4, :], got_b23[:], s_bank[1, 2][:], MULT)
-        nc.vector.tensor_tensor(yb[:, 0:2, :], got_b01[:], s_bank[1, 0][:], MULT)
+        got_a, got_b01, got_b23 = got_tile("a", PACK, 36864), got_tile("b01", 2, 40960), got_tile("b23", 2, 6144)
+        for t in range(PACK - 1):
+            look_up(got_a[:, t, :], t, 0)
+            look_up((got_b01, got_b23)[t // 2][:, t % 2, :], t, HALF)
+        for j0 in (0, CH):
+            look_up(got_a[:, PACK - 1, j0 : j0 + CH], PACK - 1, j0)
+        look_up(got_b23[:, 1, :], PACK - 1, HALF)
+        nc.vector.tensor_tensor(ya[:, :, 0:CH], got_a[:, :, 0:CH], s_bank[0, 0][:], MULT)
+        score_slots(HALF, HALF, 0, 2, "bank0")
+        nc.vector.tensor_tensor(ya[:, :, CH:HALF], got_a[:, :, CH:HALF], s_bank[CH, 0][:], MULT)
+        nc.vector.tensor_tensor(yb[:, 2:4, :], got_b23[:], s_bank[HALF, 2][:], MULT)
+        nc.vector.tensor_tensor(yb[:, 0:2, :], got_b01[:], s_bank[HALF, 0][:], MULT)
 
         def squash(th, y):
             nc.scalar.activation(

@@ -11,6 +11,7 @@ U8 = mybir.dt.uint8
 FP8X4 = mybir.dt.float8_e4m3fn_x4
 ACT = mybir.ActivationFunctionType
 MULT = mybir.AluOpType.mult
+ADD = mybir.AluOpType.add
 
 P = 128
 PACK = 4
@@ -212,7 +213,7 @@ def tile_picked_temper_tanh_p_kernel(
         ths = [P, CH, PACK]
         vcopy, scopy = nc.vector.tensor_copy, nc.scalar.copy
         w0 = ring("w0", ths, BF16, "w0")
-        weave(w0[:], w_raw[0][:, :, 0:CH], scopy)
+        nc.gpsimd.tensor_scalar(w0[:], w_raw[0][:, :, 0:CH].rearrange("p t m -> p m t"), 1.0, 0.0, MULT, ADD)
         th0 = shared.tile(ths, F32, name="th0", align_bytes=64, offset=43008)
         squash(th0[:], ya[:, :, 0:CH])
         th1 = shared.tile(ths, F32, name="th1", align_bytes=64, offset=45056)

@@ -22,6 +22,7 @@ N = 512
 U = 512
 HALF = 256
 CH = 128
+SPLIT = 192
 FLOPS = 2 * 512 * H * S + 2 * H * N * S
 
 
@@ -137,23 +138,22 @@ def tile_picked_temper_tanh_p_kernel(
 
         score_slots(0, CH, 0, PACK, "bank0")
         score_slots(CH, CH, 0, PACK, "bank1")
-        score_slots(HALF, HALF, 2, 2, "bank3")
+        score_slots(HALF, CH, 0, PACK, "bank2")
+        score_slots(HALF + CH, CH, 0, PACK, "bank3")
 
         def got_tile(label, slots, offset):
             return shared.tile([P, slots, HALF], F32, name=f"got_{label}", align_bytes=64, offset=offset)
 
-        got_a, got_b01, got_b23 = got_tile("a", PACK, 36864), got_tile("b01", 2, 40960), got_tile("b23", 2, 6144)
+        got_a, got_b = got_tile("a", PACK, 36864), got_tile("b", PACK, 4096)
         for t in range(PACK - 1):
             look_up(got_a[:, t, :], t, 0)
-            look_up((got_b01, got_b23)[t // 2][:, t % 2, :], t, HALF)
+            look_up(got_b[:, t, :], t, HALF)
         for j0 in (0, CH):
             look_up(got_a[:, PACK - 1, j0 : j0 + CH], PACK - 1, j0)
-        look_up(got_b23[:, 1, :], PACK - 1, HALF)
-        nc.vector.tensor_tensor(ya[:, :, 0:CH], got_a[:, :, 0:CH], s_bank[0, 0][:], MULT)
-        score_slots(HALF, HALF, 0, 2, "bank0")
-        nc.vector.tensor_tensor(ya[:, :, CH:HALF], got_a[:, :, CH:HALF], s_bank[CH, 0][:], MULT)
-        nc.vector.tensor_tensor(yb[:, 2:4, :], got_b23[:], s_bank[HALF, 2][:], MULT)
-        nc.vector.tensor_tensor(yb[:, 0:2, :], got_b01[:], s_bank[HALF, 0][:], MULT)
+        look_up(got_b[:, PACK - 1, :], PACK - 1, HALF)
+        for y, got, j0 in ((ya, got_a, 0), (yb, got_b, HALF)):
+            for c0 in (0, CH):
+                nc.vector.tensor_tensor(y[:, :, c0 : c0 + CH], got[:, :, c0 : c0 + CH], s_bank[j0 + c0, 0][:], MULT)
 
         def squash(th, y):
             nc.scalar.activation(
@@ -212,14 +212,15 @@ def tile_picked_temper_tanh_p_kernel(
 
         ths = [P, CH, PACK]
         vcopy, scopy = nc.vector.tensor_copy, nc.scalar.copy
-        w0 = ring("w0", ths, BF16, "w0")
-        nc.gpsimd.tensor_scalar(w0[:], w_raw[0][:, :, 0:CH].rearrange("p t m -> p m t"), 1.0, 0.0, MULT, ADD)
+        wa = ring("wa", [P, HALF, PACK], BF16, "wa")
+        nc.gpsimd.tensor_scalar(
+            wa[:, 0:SPLIT, :], w_raw[0][:, :, 0:SPLIT].rearrange("p t m -> p m t"), 1.0, 0.0, MULT, ADD
+        )
         th0 = shared.tile(ths, F32, name="th0", align_bytes=64, offset=43008)
         squash(th0[:], ya[:, :, 0:CH])
         th1 = shared.tile(ths, F32, name="th1", align_bytes=64, offset=45056)
         squash(th1[:], ya[:, :, CH:HALF])
-        w1_woven = shared.tile(ths, BF16, name="w1_woven", align_bytes=64, offset=6144)
-        weave(w1_woven[:], w_raw[0][:, :, CH:HALF], vcopy)
+        weave(wa[:, SPLIT:HALF, :], w_raw[0][:, :, SPLIT:HALF], scopy)
         th2 = shared.tile(ths, F32, name="th2", align_bytes=64, offset=47104)
         squash(th2[:], yb[:, :, 0:CH])
         wb = shared.tile([P, HALF, PACK], BF16, name="wb", align_bytes=64, offset=21504)
@@ -227,9 +228,7 @@ def tile_picked_temper_tanh_p_kernel(
         z01 = shared.tile([P, HALF, PACK], BF16, name="z01", align_bytes=64, offset=49152)
         weigh(z01[:, 0:CH, :], th0[:])
         weigh(z01[:, CH:HALF, :], th1[:])
-        qa = mx_tiles("wa", 20480)
-        quantise_into(qa, 0, w0[:])
-        quantise_into(qa, CH, w1_woven[:])
+        qa = quantise(wa[:], "wa", 20480)
         q01 = quantise(z01[:], "z01", 12288)
         th3 = shared.tile(ths, F32, name="th3", align_bytes=64, offset=49152)
         squash(th3[:], yb[:, :, CH:HALF])

@@ -254,6 +254,10 @@ def tile_picked_temper_tanh_p_kernel(
         res_b = ring("res_b", [P, PACK, HALF], F32, "res_b")
         for b0, bank, copy in ((0, "bank1", vcopy), (2, "bank2", scopy)):
             project(res_b[:, b0 : b0 + 2, 0:CH], HALF, q23, qw, b0, bank, copy)
+        store(res_b[:, 0:2, 0:CH], HALF, 0)
         for block, bank in enumerate(("bank3", "bank4", "bank5", "bank6")):
             project(res_b[:, block : block + 1, CH:HALF], HALF + CH, q23, qw, block, bank, (vcopy, scopy)[block % 2], CH)
-            store(res_b[:, block : block + 1, :], HALF, block)
+            if block == 1:
+                store(res_b[:, 0:2, CH:HALF], HALF + CH, 0)
+            if block > 1:
+                store(res_b[:, block : block + 1, :], HALF, block)

@@ -136,10 +136,9 @@ def tile_picked_temper_tanh_p_kernel(
             for e in range(slots):
                 score(s_bank[j0, t0][:, e, :], t0 + e, j0)
 
-        score_slots(0, CH, 0, PACK, "bank0")
-        score_slots(CH, CH, 0, PACK, "bank1")
-        score_slots(HALF, CH, 0, PACK, "bank2")
-        score_slots(HALF + CH, CH, 0, PACK, "bank3")
+        pieces = [(c * CH, t0, 2, f"bank{c + 2 * t0}") for c in range(3) for t0 in (0, 2)] + [(3 * CH, 0, PACK, "bank3")]
+        for piece in pieces:
+            score_slots(piece[0], CH, *piece[1:])
 
         def got_tile(label, slots, offset):
             return shared.tile([P, slots, HALF], F32, name=f"got_{label}", align_bytes=64, offset=offset)
@@ -151,9 +150,10 @@ def tile_picked_temper_tanh_p_kernel(
         for j0 in (0, CH):
             look_up(got_a[:, PACK - 1, j0 : j0 + CH], PACK - 1, j0)
         look_up(got_b[:, PACK - 1, :], PACK - 1, HALF)
-        for y, got, j0 in ((ya, got_a, 0), (yb, got_b, HALF)):
-            for c0 in (0, CH):
-                nc.vector.tensor_tensor(y[:, :, c0 : c0 + CH], got[:, :, c0 : c0 + CH], s_bank[j0 + c0, 0][:], MULT)
+        for j0, t0, slots, tag in pieces:
+            y, got = ((ya, got_a), (yb, got_b))[j0 // HALF]
+            place = (slice(None), slice(t0, t0 + slots), slice(j0 % HALF, j0 % HALF + CH))
+            nc.vector.tensor_tensor(y[place], got[place], s_bank[j0, t0][:], MULT)
 
         def squash(th, y):
             nc.scalar.activation(

@@ -66,7 +66,7 @@ def tile_picked_temper_tanh_p_kernel(
         temp_win.append(load_temp(3, 69632))
 
         dsc_got = sb.tile([P, H], U8, name="dsc_got", align_bytes=64)
-        xsc_got = sb.tile([P, S], U8, name="xsc_got", align_bytes=64)
+        xsc_got = shared.tile([P, S], U8, name="xsc_got", align_bytes=64, offset=75520)
 
         def entries(lst, j0, n):
             return lst[:, j0 // 16 : (j0 + n) // 16]
@@ -83,7 +83,7 @@ def tile_picked_temper_tanh_p_kernel(
         deal(planes[:, 0:H], dsc_got, 0, H)
         nc.vector.tensor_copy(planes[:, H : H + S].bitcast(I32), xsc_got[:].bitcast(I32))
         for r in range(1, PACK):
-            nc.scalar.dma_start(planes[r:P:32, :].bitcast(I32), planes[8 * r : P : 32, :].bitcast(I32))
+            nc.sync.dma_start(planes[r:P:32, :].bitcast(I32), planes[8 * r : P : 32, :].bitcast(I32))
 
         dw_got = shared.tile([P, H], U32, name="dw_got", align_bytes=64, offset=65536)
         dw_dealt = shared.tile([P, H], U32, name="dw_dealt", align_bytes=64, offset=16384)
@@ -96,11 +96,11 @@ def tile_picked_temper_tanh_p_kernel(
             deal(dw_dealt[:], dw_got, h * HALF, HALF)
         w_rows = w1.rearrange("(p t) m -> p t m", t=PACK)
         w_raw = [
-            shared.tile([P, PACK, HALF], F32, name="w_raw0", align_bytes=64, offset=61440),
-            shared.tile([P, PACK, HALF], F32, name="w_raw1", align_bytes=64, offset=65536),
+            shared.tile([P, PACK, HALF], F32, name="w_raw0", align_bytes=64, offset=71680),
+            shared.tile([P, PACK, HALF], F32, name="w_raw1", align_bytes=64, offset=75840),
         ]
         nc.sync.dma_start(w_raw[0][:], w_rows[:, :, 0:HALF])
-        gn_sb = shared.tile([P, PACK], F32, name="gn_sb", align_bytes=64, offset=57344)
+        gn_sb = shared.tile([P, PACK], F32, name="gn_sb", align_bytes=64, offset=75776)
         nc.sync.dma_start(gn_sb[:], gn[:, 0].rearrange("(p t) -> p t", t=PACK))
         nc.sync.dma_start(w_raw[1][:], w_rows[:, :, HALF:N])
 

@@ -1,6 +1,7 @@
 from contextlib import ExitStack
 
 import concourse.mybir as mybir
+from concourse.masks import make_identity
 
 F32 = mybir.dt.float32
 BF16 = mybir.dt.bfloat16
@@ -22,7 +23,6 @@ N = 512
 U = 512
 HALF = 256
 CH = 128
-SPLIT = 192
 FLOPS = 2 * 512 * H * S + 2 * H * N * S
 
 
@@ -43,6 +43,11 @@ def tile_picked_temper_tanh_p_kernel(
         xsc_win = sb.tile([P, TABLE], U8, name="xsc_win", align_bytes=64)
         nc.vector.memset(dsc_win[:].bitcast(I32), 0)
         nc.gpsimd.memset(xsc_win[:].bitcast(I32), 0)
+        ident = sb.tile([P, P], F32, name="ident", align_bytes=64)
+        gn_row = sb.tile([P, H], F32, name="gn_row", align_bytes=64)
+        nc.vector.memset(ident[:], 0.0)
+        nc.vector.memset(gn_row[:], 0.0)
+        make_identity(nc, ident[:], nomemset=True)
 
         dw_win = shared.tile([P, TABLE], I32, name="dw_win", align_bytes=64, offset=57344)
         xw_win = sb.tile([P, TABLE], I32, name="xw_win", align_bytes=64)
@@ -60,10 +65,15 @@ def tile_picked_temper_tanh_p_kernel(
         nc.sync.dma_start(dsc_win[0:P:8, :].bitcast(I32), d_scales[0].bitcast(I32))
         nc.sync.dma_start(xsc_win[0:P:8, :].bitcast(I32), x_scales[0].bitcast(I32))
         nc.sync.dma_start(dw_win[:], d_words[0].rearrange("p n t -> p (n t)").bitcast(I32))
+        nc.sync.dma_start(gn_row[0:1, :], gn.rearrange("h o -> o h"))
         temp_win.append(load_temp(1, 14336))
         temp_win.append(load_temp(2, 55296))
         nc.sync.dma_start(xw_win[:], x_words[0].rearrange("p n t -> p (n t)").bitcast(I32))
         temp_win.append(load_temp(3, 69632))
+
+        gn_bank = ps.tile([P, P + PACK], F32, name="gn_bank", tag="bank7")
+        for t in range(PACK):
+            nc.tensor.transpose(gn_bank[:, t : t + P], gn_row[:, t:H:PACK], ident[:])
 
         dsc_got = sb.tile([P, H], U8, name="dsc_got", align_bytes=64)
         xsc_got = shared.tile([P, S], U8, name="xsc_got", align_bytes=64, offset=75520)
@@ -100,8 +110,6 @@ def tile_picked_temper_tanh_p_kernel(
             shared.tile([P, PACK, HALF], F32, name="w_raw1", align_bytes=64, offset=75840),
         ]
         nc.sync.dma_start(w_raw[0][:], w_rows[:, :, 0:HALF])
-        gn_sb = shared.tile([P, PACK], F32, name="gn_sb", align_bytes=64, offset=75776)
-        nc.sync.dma_start(gn_sb[:], gn[:, 0].rearrange("(p t) -> p t", t=PACK))
         nc.sync.dma_start(w_raw[1][:], w_rows[:, :, HALF:N])
 
         xw_got = [
@@ -164,7 +172,7 @@ def tile_picked_temper_tanh_p_kernel(
             )
 
         def weigh(z, th):
-            nc.vector.tensor_tensor(z, th, gn_sb[:].unsqueeze(1).to_broadcast(list(th.shape)), MULT)
+            nc.vector.tensor_tensor(z, th, gn_bank[:, 0:PACK].unsqueeze(1).to_broadcast(list(th.shape)), MULT)
 
         def weave(woven, src, copy):
             copy(woven.rearrange("p (c i) t -> p c t i", i=4), src.rearrange("p t (c i) -> p c t i", i=4))
@@ -213,14 +221,11 @@ def tile_picked_temper_tanh_p_kernel(
         ths = [P, CH, PACK]
         vcopy, scopy = nc.vector.tensor_copy, nc.scalar.copy
         wa = ring("wa", [P, HALF, PACK], BF16, "wa")
-        nc.gpsimd.tensor_scalar(
-            wa[:, 0:SPLIT, :], w_raw[0][:, :, 0:SPLIT].rearrange("p t m -> p m t"), 1.0, 0.0, MULT, ADD
-        )
+        nc.gpsimd.tensor_scalar(wa[:], w_raw[0][:].rearrange("p t m -> p m t"), 1.0, 0.0, MULT, ADD)
         th0 = shared.tile(ths, F32, name="th0", align_bytes=64, offset=43008)
         squash(th0[:], ya[:, :, 0:CH])
         th1 = shared.tile(ths, F32, name="th1", align_bytes=64, offset=45056)
         squash(th1[:], ya[:, :, CH:HALF])
-        weave(wa[:, SPLIT:HALF, :], w_raw[0][:, :, SPLIT:HALF], scopy)
         th2 = shared.tile(ths, F32, name="th2", align_bytes=64, offset=47104)
         squash(th2[:], yb[:, :, 0:CH])
         wb = shared.tile([P, HALF, PACK], BF16, name="wb", align_bytes=64, offset=21504)
@@ -245,7 +250,7 @@ def tile_picked_temper_tanh_p_kernel(
             project(res[:, block : block + 1, :], 0, q01, qw, block, bank, scopy)
         store(res[:], 0, 0)
         res = shared.tile([P, 1, HALF], F32, name="res_a2", align_bytes=64, offset=45056)
-        project(res[:], 0, q01, qw, 2, "bank7", vcopy)
+        project(res[:], 0, q01, qw, 2, "bank4", vcopy)
         store(res[:], 0, 2)
         quantise_into(q23, CH, z3[:])
         res = ring("res_a3", [P, 1, HALF], F32, "res_a3")
@@ -255,7 +260,7 @@ def tile_picked_temper_tanh_p_kernel(
         for b0, bank, copy in ((0, "bank1", vcopy), (2, "bank2", scopy)):
             project(res_b[:, b0 : b0 + 2, 0:CH], HALF, q23, qw, b0, bank, copy)
         store(res_b[:, 0:2, 0:CH], HALF, 0)
-        for block, bank in enumerate(("bank3", "bank4", "bank5", "bank6")):
+        for block, bank in enumerate(("bank3", "bank5", "bank6", "bank4")):
             project(res_b[:, block : block + 1, CH:HALF], HALF + CH, q23, qw, block, bank, (vcopy, scopy)[block % 2], CH)
             if block == 1:
                 store(res_b[:, 0:2, CH:HALF], HALF + CH, 0)

@@ -136,7 +136,7 @@ def tile_picked_temper_tanh_p_kernel(
             )
 
         ya = shared.tile([P, PACK, HALF], F32, name="ya", align_bytes=64, offset=20480)
-        yb = shared.tile([P, PACK, HALF], F32, name="yb", align_bytes=64, offset=28672)
+        y2 = shared.tile([P, PACK, CH], F32, name="y2", align_bytes=64, offset=28672)
         s_bank = {}
 
         def score_slots(j0, n, t0, slots, bank_tag):
@@ -158,10 +158,14 @@ def tile_picked_temper_tanh_p_kernel(
         for j0 in (0, CH):
             look_up(got_a[:, PACK - 1, j0 : j0 + CH], PACK - 1, j0)
         look_up(got_b[:, PACK - 1, :], PACK - 1, HALF)
-        for j0, t0, slots, tag in pieces:
-            y, got = ((ya, got_a), (yb, got_b))[j0 // HALF]
-            place = (slice(None), slice(t0, t0 + slots), slice(j0 % HALF, j0 % HALF + CH))
-            nc.vector.tensor_tensor(y[place], got[place], s_bank[j0, t0][:], MULT)
+        def product(y, j0, t0, slots):
+            c0 = j0 % HALF
+            got = (got_a, got_b)[j0 // HALF]
+            nc.vector.tensor_tensor(y, got[:, t0 : t0 + slots, c0 : c0 + CH], s_bank[j0, t0][:], MULT)
+
+        for j0, t0, slots, tag in pieces[:-1]:
+            y = ya[:, :, j0 : j0 + CH] if j0 < HALF else y2[:]
+            product(y[:, t0 : t0 + slots, :], j0, t0, slots)
 
         def squash(th, y):
             nc.scalar.activation(
@@ -220,14 +224,14 @@ def tile_picked_temper_tanh_p_kernel(
 
         ths = [P, CH, PACK]
         vcopy, scopy = nc.vector.tensor_copy, nc.scalar.copy
-        wa = ring("wa", [P, HALF, PACK], BF16, "wa")
+        wa = shared.tile([P, HALF, PACK], BF16, name="wa", align_bytes=64, offset=30720)
         nc.gpsimd.tensor_scalar(wa[:], w_raw[0][:].rearrange("p t m -> p m t"), 1.0, 0.0, MULT, ADD)
         th0 = shared.tile(ths, F32, name="th0", align_bytes=64, offset=43008)
         squash(th0[:], ya[:, :, 0:CH])
         th1 = shared.tile(ths, F32, name="th1", align_bytes=64, offset=45056)
         squash(th1[:], ya[:, :, CH:HALF])
         th2 = shared.tile(ths, F32, name="th2", align_bytes=64, offset=47104)
-        squash(th2[:], yb[:, :, 0:CH])
+        squash(th2[:], y2[:])
         wb = shared.tile([P, HALF, PACK], BF16, name="wb", align_bytes=64, offset=21504)
         weave(wb[:], w_raw[1][:], scopy)
         z01 = shared.tile([P, HALF, PACK], BF16, name="z01", align_bytes=64, offset=49152)
@@ -235,34 +239,36 @@ def tile_picked_temper_tanh_p_kernel(
         weigh(z01[:, CH:HALF, :], th1[:])
         qa = quantise(wa[:], "wa", 20480)
         q01 = quantise(z01[:], "z01", 12288)
-        th3 = shared.tile(ths, F32, name="th3", align_bytes=64, offset=49152)
-        squash(th3[:], yb[:, :, CH:HALF])
-        z2 = shared.tile(ths, BF16, name="z2", align_bytes=64, offset=45056)
+        y3 = shared.tile([P, PACK, CH], F32, name="y3", align_bytes=64, offset=30720)
+        product(y3[:], HALF + CH, 0, PACK)
+        qb = mx_tiles("wb", 46080)
+        quantise_into(qb, 0, wb[:, 0:P, :])
+        z2 = shared.tile(ths, BF16, name="z2", align_bytes=64, offset=75840)
         weigh(z2[:], th2[:])
-        qb = quantise(wb[:], "wb", 46080)
+        quantise_into(qb, P, wb[:, P:HALF, :])
         qw = [(qa, 0), (qa, P), (qb, 0), (qb, P)]
         q23 = mx_tiles("z23", 36864)
         quantise_into(q23, 0, z2[:])
+        res = ring("res_a0", [P, 1, HALF], F32, "res_a0")
+        project(res[:], 0, q01, qw, 0, "bank5", scopy)
+        store(res[:], 0, 0)
+        th3 = shared.tile(ths, F32, name="th3", align_bytes=64, offset=49152)
+        squash(th3[:], y3[:])
+        res = shared.tile([P, 2, HALF], F32, name="res_a1", align_bytes=64, offset=30720)
+        for block, bank in ((1, "bank6"), (2, "bank4")):
+            project(res[:, block - 1 : block, :], 0, q01, qw, block, bank, scopy)
+        store(res[:], 0, 1)
         z3 = shared.tile(ths, BF16, name="z3", align_bytes=64, offset=47104)
         weigh(z3[:], th3[:])
-        res = ring("res_a0", [P, 2, HALF], F32, "res_a0")
-        for block, bank in ((0, "bank5"), (1, "bank6")):
-            project(res[:, block : block + 1, :], 0, q01, qw, block, bank, scopy)
-        store(res[:], 0, 0)
-        res = shared.tile([P, 1, HALF], F32, name="res_a2", align_bytes=64, offset=45056)
-        project(res[:], 0, q01, qw, 2, "bank4", vcopy)
-        store(res[:], 0, 2)
-        quantise_into(q23, CH, z3[:])
-        res = ring("res_a3", [P, 1, HALF], F32, "res_a3")
-        project(res[:], 0, q01, qw, 3, "bank0", scopy)
+        res = shared.tile([P, 1, HALF], F32, name="res_a3", align_bytes=64, offset=75840)
+        project(res[:], 0, q01, qw, 3, "bank0", vcopy)
         store(res[:], 0, 3)
+        quantise_into(q23, CH, z3[:])
         res_b = ring("res_b", [P, PACK, HALF], F32, "res_b")
-        for b0, bank, copy in ((0, "bank1", vcopy), (2, "bank2", scopy)):
+        for b0, bank, copy in ((0, "bank1", scopy), (2, "bank2", vcopy)):
             project(res_b[:, b0 : b0 + 2, 0:CH], HALF, q23, qw, b0, bank, copy)
-        store(res_b[:, 0:2, 0:CH], HALF, 0)
+            store(res_b[:, b0 : b0 + 2, 0:CH], HALF, b0)
         for block, bank in enumerate(("bank3", "bank5", "bank6", "bank4")):
             project(res_b[:, block : block + 1, CH:HALF], HALF + CH, q23, qw, block, bank, (vcopy, scopy)[block % 2], CH)
-            if block == 1:
-                store(res_b[:, 0:2, CH:HALF], HALF + CH, 0)
-            if block > 1:
-                store(res_b[:, block : block + 1, :], HALF, block)
+            if block % 2:
+                store(res_b[:, block - 1 : block + 1, CH:HALF], HALF + CH, block - 1)

@@ -23,6 +23,7 @@ N = 512
 U = 512
 HALF = 256
 CH = 128
+EARLY = 64
 FLOPS = 2 * 512 * H * S + 2 * H * N * S
 
 
@@ -158,14 +159,16 @@ def tile_picked_temper_tanh_p_kernel(
         for j0 in (0, CH):
             look_up(got_a[:, PACK - 1, j0 : j0 + CH], PACK - 1, j0)
         look_up(got_b[:, PACK - 1, :], PACK - 1, HALF)
-        def product(y, j0, t0, slots):
-            c0 = j0 % HALF
+        def product(y, j0, t0, slots, first=0):
+            c0, n = j0 % HALF + first, y.shape[2]
             got = (got_a, got_b)[j0 // HALF]
-            nc.vector.tensor_tensor(y, got[:, t0 : t0 + slots, c0 : c0 + CH], s_bank[j0, t0][:], MULT)
+            nc.vector.tensor_tensor(y, got[:, t0 : t0 + slots, c0 : c0 + n], s_bank[j0, t0][:, :, first : first + n], MULT)
 
         for j0, t0, slots, tag in pieces[:-1]:
             y = ya[:, :, j0 : j0 + CH] if j0 < HALF else y2[:]
             product(y[:, t0 : t0 + slots, :], j0, t0, slots)
+        y3_early = sb.tile([P, PACK, EARLY], F32, name="y3_early", align_bytes=64)
+        product(y3_early[:], HALF + CH, 0, PACK)
 
         def squash(th, y):
             nc.scalar.activation(
@@ -239,8 +242,11 @@ def tile_picked_temper_tanh_p_kernel(
         weigh(z01[:, CH:HALF, :], th1[:])
         qa = quantise(wa[:], "wa", 20480)
         q01 = quantise(z01[:], "z01", 12288)
-        y3 = shared.tile([P, PACK, CH], F32, name="y3", align_bytes=64, offset=30720)
-        product(y3[:], HALF + CH, 0, PACK)
+        y3 = shared.tile([P, PACK, CH - EARLY], F32, name="y3", align_bytes=64, offset=30720)
+        product(y3[:], HALF + CH, 0, PACK, EARLY)
+        th3 = shared.tile(ths, F32, name="th3", align_bytes=64, offset=76864)
+        squash(th3[:, 0:EARLY, :], y3_early[:])
+        squash(th3[:, EARLY:CH, :], y3[:])
         qb = mx_tiles("wb", 46080)
         quantise_into(qb, 0, wb[:, 0:P, :])
         z2 = shared.tile(ths, BF16, name="z2", align_bytes=64, offset=75840)
@@ -252,13 +258,11 @@ def tile_picked_temper_tanh_p_kernel(
         res = ring("res_a0", [P, 1, HALF], F32, "res_a0")
         project(res[:], 0, q01, qw, 0, "bank5", scopy)
         store(res[:], 0, 0)
-        th3 = shared.tile(ths, F32, name="th3", align_bytes=64, offset=49152)
-        squash(th3[:], y3[:])
-        res = shared.tile([P, 2, HALF], F32, name="res_a1", align_bytes=64, offset=30720)
+        res = ring("res_a1", [P, 2, HALF], F32, "res_a1")
         for block, bank in ((1, "bank6"), (2, "bank4")):
             project(res[:, block - 1 : block, :], 0, q01, qw, block, bank, scopy)
         store(res[:], 0, 1)
-        z3 = shared.tile(ths, BF16, name="z3", align_bytes=64, offset=47104)
+        z3 = shared.tile(ths, BF16, name="z3", align_bytes=64, offset=21504)
         weigh(z3[:], th3[:])
         res = shared.tile([P, 1, HALF], F32, name="res_a3", align_bytes=64, offset=75840)
         project(res[:], 0, q01, qw, 3, "bank0", vcopy)

@@ -107,11 +107,12 @@ def tile_picked_temper_tanh_p_kernel(
             deal(dw_dealt[:], dw_got, h * HALF, HALF)
         w_rows = w1.rearrange("(p t) m -> p t m", t=PACK)
         w_raw = [
-            shared.tile([P, PACK, HALF], F32, name="w_raw0", align_bytes=64, offset=71680),
-            shared.tile([P, PACK, HALF], F32, name="w_raw1", align_bytes=64, offset=75840),
+            shared.tile([P, PACK, HALF], F32, name="w_raw0", align_bytes=64, offset=71744),
+            shared.tile([P, PACK, P], F32, name="w_raw2", align_bytes=64, offset=75840),
+            shared.tile([P, PACK, P], F32, name="w_raw3", align_bytes=64, offset=65536),
         ]
-        nc.sync.dma_start(w_raw[0][:], w_rows[:, :, 0:HALF])
-        nc.sync.dma_start(w_raw[1][:], w_rows[:, :, HALF:N])
+        for raw, m0 in zip(w_raw, (0, HALF, HALF + P)):
+            nc.sync.dma_start(raw[:], w_rows[:, :, m0 : m0 + raw.shape[2]])
 
         xw_got = [
             shared.tile([P, HALF], U32, name=f"xw_got{h}", align_bytes=64, offset=51200 + 2048 * h) for h in range(2)
@@ -227,7 +228,7 @@ def tile_picked_temper_tanh_p_kernel(
 
         ths = [P, CH, PACK]
         vcopy, scopy = nc.vector.tensor_copy, nc.scalar.copy
-        wa = shared.tile([P, HALF, PACK], BF16, name="wa", align_bytes=64, offset=30720)
+        wa = shared.tile([P, HALF, PACK], BF16, name="wa", align_bytes=64, offset=77888)
         nc.gpsimd.tensor_scalar(wa[:], w_raw[0][:].rearrange("p t m -> p m t"), 1.0, 0.0, MULT, ADD)
         th0 = shared.tile(ths, F32, name="th0", align_bytes=64, offset=43008)
         squash(th0[:], ya[:, :, 0:CH])
@@ -236,20 +237,21 @@ def tile_picked_temper_tanh_p_kernel(
         th2 = shared.tile(ths, F32, name="th2", align_bytes=64, offset=47104)
         squash(th2[:], y2[:])
         wb = shared.tile([P, HALF, PACK], BF16, name="wb", align_bytes=64, offset=21504)
-        weave(wb[:], w_raw[1][:], scopy)
+        for e in range(2):
+            weave(wb[:, e * P : (e + 1) * P, :], w_raw[1 + e][:], scopy)
         z01 = shared.tile([P, HALF, PACK], BF16, name="z01", align_bytes=64, offset=49152)
         weigh(z01[:, 0:CH, :], th0[:])
         weigh(z01[:, CH:HALF, :], th1[:])
         qa = quantise(wa[:], "wa", 20480)
         q01 = quantise(z01[:], "z01", 12288)
-        y3 = shared.tile([P, PACK, CH - EARLY], F32, name="y3", align_bytes=64, offset=30720)
+        y3 = shared.tile([P, PACK, CH - EARLY], F32, name="y3", align_bytes=64, offset=78912)
         product(y3[:], HALF + CH, 0, PACK, EARLY)
-        th3 = shared.tile(ths, F32, name="th3", align_bytes=64, offset=76864)
+        th3 = shared.tile(ths, F32, name="th3", align_bytes=64, offset=65536)
         squash(th3[:, 0:EARLY, :], y3_early[:])
         squash(th3[:, EARLY:CH, :], y3[:])
         qb = mx_tiles("wb", 46080)
         quantise_into(qb, 0, wb[:, 0:P, :])
-        z2 = shared.tile(ths, BF16, name="z2", align_bytes=64, offset=75840)
+        z2 = shared.tile(ths, BF16, name="z2", align_bytes=64, offset=77376)
         weigh(z2[:], th2[:])
         quantise_into(qb, P, wb[:, P:HALF, :])
         qw = [(qa, 0), (qa, P), (qb, 0), (qb, P)]
@@ -264,14 +266,14 @@ def tile_picked_temper_tanh_p_kernel(
         store(res[:], 0, 1)
         z3 = shared.tile(ths, BF16, name="z3", align_bytes=64, offset=21504)
         weigh(z3[:], th3[:])
-        res = shared.tile([P, 1, HALF], F32, name="res_a3", align_bytes=64, offset=75840)
+        res = shared.tile([P, 1, HALF], F32, name="res_a3", align_bytes=64, offset=77376)
         project(res[:], 0, q01, qw, 3, "bank0", vcopy)
         store(res[:], 0, 3)
         quantise_into(q23, CH, z3[:])
         res_b = ring("res_b", [P, PACK, HALF], F32, "res_b")
         for b0, bank, copy in ((0, "bank1", scopy), (2, "bank2", vcopy)):
             project(res_b[:, b0 : b0 + 2, 0:CH], HALF, q23, qw, b0, bank, copy)
-            store(res_b[:, b0 : b0 + 2, 0:CH], HALF, b0)
+        store(res_b[:, :, 0:CH], HALF, 0)
         for block, bank in enumerate(("bank3", "bank5", "bank6", "bank4")):
             project(res_b[:, block : block + 1, CH:HALF], HALF + CH, q23, qw, block, bank, (vcopy, scopy)[block % 2], CH)
             if block % 2:

from contextlib import ExitStack

import concourse.mybir as mybir
from concourse.masks import make_identity

F32 = mybir.dt.float32
BF16 = mybir.dt.bfloat16
I32 = mybir.dt.int32
U32 = mybir.dt.uint32
U16 = mybir.dt.uint16
U8 = mybir.dt.uint8
FP8X4 = mybir.dt.float8_e4m3fn_x4
ACT = mybir.ActivationFunctionType
MULT = mybir.AluOpType.mult
ADD = mybir.AluOpType.add

P = 128
PACK = 4
TABLE = 2048
S = 512
H = 512
N = 512
U = 512
HALF = 256
CH = 128
EARLY = 64
FLOPS = 2 * 512 * H * S + 2 * H * N * S


def tile_picked_temper_tanh_p_kernel(
    tc, x_words, x_scales, d_words, d_scales, temp, gn, w1, offs, kidx, task, out
):
    nc = tc.nc
    with ExitStack() as ctx:
        lists = ctx.enter_context(tc.tile_pool(name="lists", bufs=1))
        sb = ctx.enter_context(tc.tile_pool(name="sb", bufs=1))
        shared = ctx.enter_context(tc.tile_pool(name="shared", bufs=1))
        ps = ctx.enter_context(tc.psum_pool(name="ps", bufs=1))

        kidx_sb = lists.tile([P, H // 16], U16, name="kidx_sb")
        offs_sb = lists.tile([P, S // 16], U16, name="offs_sb")
        task_sb = lists.tile([P, S // 16], U16, name="task_sb")
        dsc_win = sb.tile([P, TABLE], U8, name="dsc_win", align_bytes=64)
        xsc_win = sb.tile([P, TABLE], U8, name="xsc_win", align_bytes=64)
        nc.vector.memset(dsc_win[:].bitcast(I32), 0)
        nc.gpsimd.memset(xsc_win[:].bitcast(I32), 0)
        ident = sb.tile([P, P], F32, name="ident", align_bytes=64)
        gn_row = sb.tile([P, H], F32, name="gn_row", align_bytes=64)
        nc.vector.memset(ident[:], 0.0)
        nc.vector.memset(gn_row[:], 0.0)
        make_identity(nc, ident[:], nomemset=True)

        dw_win = shared.tile([P, TABLE], I32, name="dw_win", align_bytes=64, offset=57344)
        xw_win = sb.tile([P, TABLE], I32, name="xw_win", align_bytes=64)
        temp_rows = temp.rearrange("(p t) u -> p t u", t=PACK)

        def load_temp(t, offset):
            win = shared.tile([P, U], F32, name=f"temp_win{t}", align_bytes=64, offset=offset)
            nc.sync.dma_start(win[:], temp_rows[:, t, :])
            return win

        nc.sync.dma_start(task_sb[:], task)
        temp_win = [load_temp(0, 12288)]
        nc.sync.dma_start(kidx_sb[:], kidx)
        nc.sync.dma_start(offs_sb[:], offs)
        nc.sync.dma_start(dsc_win[0:P:8, :].bitcast(I32), d_scales[0].bitcast(I32))
        nc.sync.dma_start(xsc_win[0:P:8, :].bitcast(I32), x_scales[0].bitcast(I32))
        nc.sync.dma_start(dw_win[:], d_words[0].rearrange("p n t -> p (n t)").bitcast(I32))
        nc.sync.dma_start(gn_row[0:1, :], gn.rearrange("h o -> o h"))
        temp_win.append(load_temp(1, 14336))
        temp_win.append(load_temp(2, 55296))
        nc.sync.dma_start(xw_win[:], x_words[0].rearrange("p n t -> p (n t)").bitcast(I32))
        temp_win.append(load_temp(3, 69632))

        gn_bank = ps.tile([P, P + PACK], F32, name="gn_bank", tag="bank7")
        for t in range(PACK):
            nc.tensor.transpose(gn_bank[:, t : t + P], gn_row[:, t:H:PACK], ident[:])

        dsc_got = sb.tile([P, H], U8, name="dsc_got", align_bytes=64)
        xsc_got = shared.tile([P, S], U8, name="xsc_got", align_bytes=64, offset=75520)

        def entries(lst, j0, n):
            return lst[:, j0 // 16 : (j0 + n) // 16]

        def deal(dealt, got, key0, keys):
            nc.vector.tensor_copy(
                dealt.rearrange("p (t m) -> p m t", t=PACK)[:, key0 // PACK : (key0 + keys) // PACK, :],
                got[:, key0 : key0 + keys].rearrange("p (m t) -> p m t", t=PACK),
            )

        nc.vector.tensor_copy(dsc_got[:], dsc_win[:].indirect(kidx_sb[:]))
        nc.vector.tensor_copy(xsc_got[:], xsc_win[:].indirect(offs_sb[:]))
        planes = sb.tile([P, H + S], U8, name="planes", tag="xsc_win", align_bytes=64)
        deal(planes[:, 0:H], dsc_got, 0, H)
        nc.vector.tensor_copy(planes[:, H : H + S].bitcast(I32), xsc_got[:].bitcast(I32))
        for r in range(1, PACK):
            nc.sync.dma_start(planes[r:P:32, :].bitcast(I32), planes[8 * r : P : 32, :].bitcast(I32))

        dw_got = shared.tile([P, H], U32, name="dw_got", align_bytes=64, offset=65536)
        dw_dealt = shared.tile([P, H], U32, name="dw_dealt", align_bytes=64, offset=16384)
        for h in range(2):
            nc.vector.tensor_copy(
                dw_got[:, h * HALF : (h + 1) * HALF],
                dw_win[:].bitcast(U32).indirect(entries(kidx_sb, h * HALF, HALF)),
            )
        for h in range(2):
            deal(dw_dealt[:], dw_got, h * HALF, HALF)
        w_rows = w1.rearrange("(p t) m -> p t m", t=PACK)
        w_raw = [
            shared.tile([P, PACK, HALF], F32, name="w_raw0", align_bytes=64, offset=71744),
            shared.tile([P, PACK, P], F32, name="w_raw2", align_bytes=64, offset=75840),
            shared.tile([P, PACK, P], F32, name="w_raw3", align_bytes=64, offset=65536),
        ]
        for raw, m0 in zip(w_raw, (0, HALF, HALF + P)):
            nc.sync.dma_start(raw[:], w_rows[:, :, m0 : m0 + raw.shape[2]])

        xw_got = [
            shared.tile([P, HALF], U32, name=f"xw_got{h}", align_bytes=64, offset=51200 + 2048 * h) for h in range(2)
        ]
        for j0, n in ((0, CH), (CH, CH), (HALF, HALF)):
            nc.vector.tensor_copy(
                xw_got[j0 // HALF][:, j0 % HALF : j0 % HALF + n], xw_win[:].bitcast(U32).indirect(entries(offs_sb, j0, n))
            )

        def look_up(got, t, j0):
            nc.scalar.activation(got, temp_win[t][:].indirect(entries(task_sb, j0, got.shape[1])), ACT.Copy)

        def score(dst, t, j0):
            n = dst.shape[1]
            nc.tensor.matmul_mx(
                out=dst,
                lhsT=dw_dealt[:, t * P : (t + 1) * P].bitcast(FP8X4),
                lhsT_scale=planes[:, t * P : (t + 1) * P],
                rhs=xw_got[j0 // HALF][:, j0 % HALF : j0 % HALF + n].bitcast(FP8X4),
                rhs_scale=planes[:, H + j0 : H + j0 + n],
                start=True,
                stop=True,
            )

        ya = shared.tile([P, PACK, HALF], F32, name="ya", align_bytes=64, offset=20480)
        y2 = shared.tile([P, PACK, CH], F32, name="y2", align_bytes=64, offset=28672)
        s_bank = {}

        def score_slots(j0, n, t0, slots, bank_tag):
            s_bank[j0, t0] = ps.tile([P, slots, n], F32, name=f"s_bank{j0}_{t0}", tag=bank_tag)
            for e in range(slots):
                score(s_bank[j0, t0][:, e, :], t0 + e, j0)

        pieces = [(c * CH, t0, 2, f"bank{c + 2 * t0}") for c in range(3) for t0 in (0, 2)] + [(3 * CH, 0, PACK, "bank3")]
        for piece in pieces:
            score_slots(piece[0], CH, *piece[1:])

        def got_tile(label, slots, offset):
            return shared.tile([P, slots, HALF], F32, name=f"got_{label}", align_bytes=64, offset=offset)

        got_a, got_b = got_tile("a", PACK, 36864), got_tile("b", PACK, 4096)
        for t in range(PACK - 1):
            look_up(got_a[:, t, :], t, 0)
            look_up(got_b[:, t, :], t, HALF)
        for j0 in (0, CH):
            look_up(got_a[:, PACK - 1, j0 : j0 + CH], PACK - 1, j0)
        look_up(got_b[:, PACK - 1, :], PACK - 1, HALF)
        def product(y, j0, t0, slots, first=0):
            c0, n = j0 % HALF + first, y.shape[2]
            got = (got_a, got_b)[j0 // HALF]
            nc.vector.tensor_tensor(y, got[:, t0 : t0 + slots, c0 : c0 + n], s_bank[j0, t0][:, :, first : first + n], MULT)

        for j0, t0, slots, tag in pieces[:-1]:
            y = ya[:, :, j0 : j0 + CH] if j0 < HALF else y2[:]
            product(y[:, t0 : t0 + slots, :], j0, t0, slots)
        y3_early = sb.tile([P, PACK, EARLY], F32, name="y3_early", align_bytes=64)
        product(y3_early[:], HALF + CH, 0, PACK)

        def squash(th, y):
            nc.scalar.activation(
                th.rearrange("p (c i) t -> p c t i", i=4),
                y.rearrange("p t (c i) -> p c t i", i=4),
                ACT.Tanh,
                scale=0.0625,
            )

        def weigh(z, th):
            nc.vector.tensor_tensor(z, th, gn_bank[:, 0:PACK].unsqueeze(1).to_broadcast(list(th.shape)), MULT)

        def weave(woven, src, copy):
            copy(woven.rearrange("p (c i) t -> p c t i", i=4), src.rearrange("p t (c i) -> p c t i", i=4))

        def mx_tiles(label, offset):
            codes = shared.tile([P, HALF], U32, name=f"codes_{label}", align_bytes=64, offset=offset)
            scales = sb.tile([P, HALF], U8, name=f"scales_{label}", align_bytes=64)
            return codes, scales

        def quantise_into(q, c0, woven):
            cols = slice(c0, c0 + woven.shape[1])
            nc.vector.quantize_mx(
                out=q[0][:, cols].bitcast(FP8X4), scales=q[1][:, cols], in_=woven.rearrange("p n t -> p (n t)")
            )

        def quantise(woven, label, offset):
            q = mx_tiles(label, offset)
            quantise_into(q, 0, woven)
            return q

        out_rows = out.rearrange("(b p) j -> p b j", p=P)

        def project(res, j0, z_q, w_qs, b0, bank_tag, copy, c0=0):
            blocks, n = res.shape[1], res.shape[2]
            bank = ps.tile([P, blocks, n], F32, name=f"o_bank{j0}_{b0}", tag=bank_tag)
            for e in range(blocks):
                w_q, m0 = w_qs[b0 + e]
                nc.tensor.matmul_mx(
                    out=bank[:, e, :],
                    lhsT=w_q[0][:, m0 : m0 + P].bitcast(FP8X4),
                    lhsT_scale=w_q[1][:, m0 : m0 + P],
                    rhs=z_q[0][:, c0 : c0 + n].bitcast(FP8X4),
                    rhs_scale=z_q[1][:, c0 : c0 + n],
                    start=True,
                    stop=True,
                )
            copy(res, bank[:])

        def store(res, j0, b0):
            blocks, n = res.shape[1], res.shape[2]
            nc.sync.dma_start(out_rows[:, b0 : b0 + blocks, j0 : j0 + n], res)

        def ring(tag, shape, dtype, name):
            return sb.tile(shape, dtype, name=name, tag=tag, align_bytes=64)

        ths = [P, CH, PACK]
        vcopy, scopy = nc.vector.tensor_copy, nc.scalar.copy
        wa = shared.tile([P, HALF, PACK], BF16, name="wa", align_bytes=64, offset=77888)
        nc.gpsimd.tensor_scalar(wa[:], w_raw[0][:].rearrange("p t m -> p m t"), 1.0, 0.0, MULT, ADD)
        th0 = shared.tile(ths, F32, name="th0", align_bytes=64, offset=43008)
        squash(th0[:], ya[:, :, 0:CH])
        th1 = shared.tile(ths, F32, name="th1", align_bytes=64, offset=45056)
        squash(th1[:], ya[:, :, CH:HALF])
        th2 = shared.tile(ths, F32, name="th2", align_bytes=64, offset=47104)
        squash(th2[:], y2[:])
        wb = shared.tile([P, HALF, PACK], BF16, name="wb", align_bytes=64, offset=21504)
        for e in range(2):
            weave(wb[:, e * P : (e + 1) * P, :], w_raw[1 + e][:], scopy)
        z01 = shared.tile([P, HALF, PACK], BF16, name="z01", align_bytes=64, offset=49152)
        weigh(z01[:, 0:CH, :], th0[:])
        weigh(z01[:, CH:HALF, :], th1[:])
        qa = quantise(wa[:], "wa", 20480)
        q01 = quantise(z01[:], "z01", 12288)
        y3 = shared.tile([P, PACK, CH - EARLY], F32, name="y3", align_bytes=64, offset=78912)
        product(y3[:], HALF + CH, 0, PACK, EARLY)
        th3 = shared.tile(ths, F32, name="th3", align_bytes=64, offset=65536)
        squash(th3[:, 0:EARLY, :], y3_early[:])
        squash(th3[:, EARLY:CH, :], y3[:])
        qb = mx_tiles("wb", 46080)
        quantise_into(qb, 0, wb[:, 0:P, :])
        z2 = shared.tile(ths, BF16, name="z2", align_bytes=64, offset=77376)
        weigh(z2[:], th2[:])
        quantise_into(qb, P, wb[:, P:HALF, :])
        qw = [(qa, 0), (qa, P), (qb, 0), (qb, P)]
        q23 = mx_tiles("z23", 36864)
        quantise_into(q23, 0, z2[:])
        res = ring("res_a0", [P, 1, HALF], F32, "res_a0")
        project(res[:], 0, q01, qw, 0, "bank5", scopy)
        store(res[:], 0, 0)
        res = ring("res_a1", [P, 2, HALF], F32, "res_a1")
        for block, bank in ((1, "bank6"), (2, "bank4")):
            project(res[:, block - 1 : block, :], 0, q01, qw, block, bank, scopy)
        store(res[:], 0, 1)
        z3 = shared.tile(ths, BF16, name="z3", align_bytes=64, offset=21504)
        weigh(z3[:], th3[:])
        res = shared.tile([P, 1, HALF], F32, name="res_a3", align_bytes=64, offset=77376)
        project(res[:], 0, q01, qw, 3, "bank0", vcopy)
        store(res[:], 0, 3)
        quantise_into(q23, CH, z3[:])
        res_b = ring("res_b", [P, PACK, HALF], F32, "res_b")
        for b0, bank, copy in ((0, "bank1", scopy), (2, "bank2", vcopy)):
            project(res_b[:, b0 : b0 + 2, 0:CH], HALF, q23, qw, b0, bank, copy)
        store(res_b[:, :, 0:CH], HALF, 0)
        for block, bank in enumerate(("bank3", "bank5", "bank6", "bank4")):
            project(res_b[:, block : block + 1, CH:HALF], HALF + CH, q23, qw, block, bank, (vcopy, scopy)[block % 2], CH)
            if block % 2:
                store(res_b[:, block - 1 : block + 1, CH:HALF], HALF + CH, block - 1)
